import numpy as np
import ml_dtypes


def mxq(x, axis, fmt="e4m3"):
    dtype, down = {"e4m3": (ml_dtypes.float8_e4m3fn, 7), "e5m2": (ml_dtypes.float8_e5m2, 14)}[fmt]
    v = np.moveaxis(np.asarray(x, np.float32).astype(ml_dtypes.bfloat16).astype(np.float64), axis, -1)
    blocks = v.reshape(v.shape[:-1] + (-1, 32))
    amax = np.abs(blocks).max(-1, keepdims=True)
    byte = np.maximum(np.where(amax > 0, np.frexp(amax)[1] - 1 + 127, 0) - down, 1)
    scale = np.exp2(byte - 127.0)
    codes = (blocks / scale).astype(np.float32).astype(dtype).astype(np.float64)
    return np.moveaxis((codes * scale).reshape(v.shape), -1, axis)


WIDE = False


def mx_kscale(k):
    if not WIDE:
        return np.ones(k)
    levels = np.array([10, -10, 5, -5, 0])
    if k % 512:
        return np.exp2(np.random.permutation(np.resize(levels, k // 32))).repeat(32)
    a = np.empty((k // 512, 16))
    for p in range(k // 512):
        a[p, :8] = np.random.permutation(np.resize(levels, 8))
        for g in range(8):
            far = levels[np.abs(levels - a[p, g]) >= 10]
            a[p, g + 8] = far[np.random.randint(len(far))]
    return np.exp2(a.ravel()).repeat(32)


def f64(x):
    return np.asarray(x).astype(np.float64)


def striped(idx):
    return np.tile(idx.reshape(-1, 16).T, (8, 1)).astype(np.uint16)


def unstriped(offs):
    return offs[:16].T.reshape(-1).astype(np.int64)


E2M1 = np.array([0.0, 0.5, 1.0, 1.5, 2.0, 3.0, 4.0, 6.0, -0.0, -0.5, -1.0, -1.5, -2.0, -3.0, -4.0, -6.0])


def pack_weight(w, fmt):
    k, n = w.shape
    w = f64(np.asarray(w, np.float32).astype(ml_dtypes.bfloat16)).reshape(k // 32, 32, n)
    amax = np.abs(w).max(1)
    if fmt == "e4m3":
        byte = np.frexp(amax)[1] - 1 + 127 - 7
    else:
        mant, ex = np.frexp(amax / 6.0)
        byte = np.where(mant > 0.5, ex, ex - 1) + 127
    byte = np.clip(np.where(amax > 0, byte, 1), 1, 254)
    scaled = (w * np.exp2(127.0 - byte)[:, None, :]).reshape(k, n).astype(np.float32)
    by_word = np.ascontiguousarray(scaled.reshape(k // 512, 128, 4, n).transpose(0, 1, 3, 2))
    if fmt == "e4m3":
        words = by_word.astype(ml_dtypes.float8_e4m3fn).view(np.uint8)
    else:
        c = by_word.astype(ml_dtypes.float4_e2m1fn).view(np.uint8) & 0xF
        words = (c[..., 0::2] | (c[..., 1::2] << 4)).reshape(k // 512, 128, 2 * n)
    return np.ascontiguousarray(words), np.ascontiguousarray(byte.astype(np.uint8).reshape(k // 512, 16, n))


def unpack_weight(words, scales, fmt):
    g, _, n = scales.shape
    words = np.ascontiguousarray(words).reshape(g, 128, n, -1)
    if fmt == "e4m3":
        vals = words.view(ml_dtypes.float8_e4m3fn).astype(np.float64)
    else:
        nib = np.empty((g, 128, n, 4), np.uint8)
        nib[..., 0::2] = words & 0xF
        nib[..., 1::2] = words >> 4
        vals = E2M1[nib]
    vals = vals * np.repeat(np.exp2(scales.astype(np.float64) - 127.0), 8, axis=1)[..., None]
    return vals.transpose(0, 1, 3, 2).reshape(g * 512, n)


K, T, E, C, N = 512, 1280, 8, 128, 512


def by_expert(wq, xq):
    return np.concatenate([wq[e].T @ xq[:, e * C:(e + 1) * C] for e in range(E)], axis=1)


def setup_inputs():
    n = np.random.standard_normal
    s = mx_kscale(K)[:, None]
    w = [pack_weight(m, "e2m1") for m in n((E, K, N)) / np.sqrt(K) / s[None]]
    return {
        "xT": (n((K, T)) * s).astype(np.float32),
        "xr": n((N, T)).astype(np.float32),
        "w_words": np.stack([m[0] for m in w]),
        "w_scales": np.stack([m[1] for m in w]),
        "gate": np.tile(np.random.uniform(0.2, 1.0, E * C), (N, 1)).astype(np.float32),
        "offs": striped(np.random.permutation(T)[:E * C]),
    }


def reference(xT, xr, w_words, w_scales, gate, offs):
    idx = unstriped(offs)
    w = np.stack([unpack_weight(w_words[e], w_scales[e], "e2m1") for e in range(E)])
    xq = mxq(f64(xT)[:, idx], 0, "e4m3")
    y = by_expert(w, xq)
    out = f64(xr).copy()
    out[:, idx] += f64(gate) * y
    return out

@@ -1,0 +1,260 @@
+from contextlib import ExitStack
+
+import concourse.mybir as mybir
+from concourse.masks import make_identity
+
+K, T, E, C, N = 512, 1280, 8, 128, 512
+FLOPS = 2 * K * N * E * C
+BYTES = 4 * (K * T + 2 * N * T + E * C) + E * K * N // 2 + E * 16 * N + 2 * E * C
+
+P = 128
+F32 = mybir.dt.float32
+BF16 = mybir.dt.bfloat16
+I32 = mybir.dt.int32
+U32 = mybir.dt.uint32
+U16 = mybir.dt.uint16
+U8 = mybir.dt.uint8
+E4M3 = mybir.dt.float8_e4m3fn_x4
+E2M1 = mybir.dt.float4_e2m1fn_x4
+COPY = mybir.ActivationFunctionType.Copy
+ADD = mybir.AluOpType.add
+MULT = mybir.AluOpType.mult
+
+TILES = N // P
+GROUP = 2
+SPAN = GROUP * C
+PIECES = [(0, 512), (512, 384)]
+CHUNKS = [(0, 640), (640, 640)]
+
+
+def tile_moe_res_lin_none_kernel(tc, xT, xr, w_words, w_scales, gate, offs, out):
+    nc = tc.nc
+    with ExitStack() as ctx:
+        held = ctx.enter_context(tc.tile_pool(name="held", bufs=1))
+        psum = ctx.enter_context(tc.psum_pool(name="psum", bufs=4))
+
+        offsets = held.tile([P, E * C // 16], U16, name="offsets")
+
+        x_rows = xT.rearrange("(p j) t -> p j t", j=4)
+        raw = []
+        for t0, width in CHUNKS:
+            chunk = held.tile([P, 2, width], F32, name=f"raw_{t0}")
+            nc.sync.dma_start(chunk[:], x_rows[:, 0:2, t0 : t0 + width])
+            raw.append((t0, width, chunk))
+            if t0 == 0:
+                nc.sync.dma_start(offsets[:], offs)
+        scale_rows = w_scales.rearrange("e a q n -> (e a) q n")
+
+        def load_scales(e0, count):
+            rows = held.tile([P, count, N], U8, name=f"scales_w{e0}", align_bytes=64)
+            nc.gpsimd.memset(rows[:].rearrange("p e n -> p (e n)").bitcast(I32), 0)
+            for quad in range(4):
+                nc.sync.dma_start(
+                    rows[32 * quad : 32 * quad + 4].bitcast(I32),
+                    scale_rows[e0 : e0 + count, 4 * quad : 4 * quad + 4, :].bitcast(I32).rearrange("e q n -> q e n"),
+                )
+            for k in range(count):
+                scales_w[e0 + k] = rows[:, k, :]
+
+        scales_w = {}
+        load_scales(0, GROUP)
+        late = []
+        for j in range(2):
+            late_plane = held.tile([P, T], F32, name=f"late{j}")
+            nc.sync.dma_start(late_plane[:], x_rows[:, 2 + j, :])
+            late.append(late_plane)
+
+        ident = held.tile([P, P], F32, name="ident")
+        make_identity(nc, ident[:])
+        word_rows = w_words.rearrange("e a p b -> (e a) p b")
+        words = []
+        for e0 in range(0, E, GROUP):
+            group_words = held.tile([P, GROUP, 2 * N], U8, name=f"words{e0}", align_bytes=64)
+            nc.sync.dma_start(
+                group_words[:].bitcast(I32),
+                word_rows[e0 : e0 + GROUP].bitcast(I32).rearrange("e p b -> p e b"),
+            )
+            words.append(group_words)
+            if e0 == 0:
+                gate_wide = held.tile([P, 2 * SPAN], F32, name="gate_wide")
+                nc.sync.dma_start(gate_wide[:], gate[0:P, 0 : 2 * SPAN])
+                load_scales(GROUP, E - GROUP)
+                gate_rows = held.tile([P, P], F32, name="gate_rows")
+                nc.gpsimd.memset(gate_rows[:], 0.0)
+                nc.sync.dma_start(gate_rows[0:E, :], gate[0:1, :].rearrange("r (e c) -> (r e) c", e=E))
+        residual = []
+        for i in range(TILES):
+            xr_tile = held.tile([P, T], F32, name=f"xr{i}")
+            nc.sync.dma_start(xr_tile[:], xr[i * P : (i + 1) * P, :])
+            residual.append(xr_tile)
+
+        windows = []
+        for i in range(TILES):
+            window = held.tile([P, T], F32, name=f"window{i}")
+            (nc.vector if i < 2 else nc.gpsimd).memset(window[:], 0.0)
+            windows.append(window)
+
+        pairs = held.tile([P, T, 2], BF16, name="pairs", align_bytes=64)
+        gated = {}
+
+        def listed(group, count=1):
+            return offsets[:, group * SPAN // 16 : (group + count) * SPAN // 16]
+
+        def gather_pairs(group, count, target):
+            window = pairs[:].rearrange("p t j -> p (t j)").bitcast(U32)
+            slots = target.bitcast(U32).rearrange("p (s u) -> p s u", u=2)
+            nc.vector.tensor_copy(slots[:, :, 0], window.indirect(listed(group, count)))
+
+        def gather_raw(group, target, j):
+            slots = target.rearrange("p (s j) -> p s j", j=4)[:, :, 2 + j]
+            nc.vector.tensor_copy(slots, late[j][:].indirect(listed(group)))
+
+        def gather_plane(group, target, j, plane):
+            slots = target.rearrange("p (s j) -> p s j", j=4)[:, :, 2 + j]
+            nc.scalar.activation(slots, plane[:].indirect(listed(group)), COPY)
+
+        def quantise(group, count, source):
+            codes = held.tile([P, count * SPAN], U32, name=f"codes{group}", tag="early" if group == 0 else f"codes{group}", align_bytes=64)
+            scales = held.tile([P, count * SPAN], U8, name=f"scales{group}", align_bytes=64)
+            nc.vector.quantize_mx(out=codes[:].bitcast(E4M3), scales=scales[:], in_=source)
+            return codes, scales
+
+        def multiply(group, codes, scales, place):
+            banks = []
+            for k in range(GROUP):
+                cols = slice((GROUP * place + k) * C, (GROUP * place + k + 1) * C)
+                acc = psum.tile([P, N], F32, name="acc", bufs=4)
+                nc.tensor.matmul_mx(
+                    out=acc[:],
+                    lhsT=codes[:, cols].bitcast(E4M3),
+                    lhsT_scale=scales[:, cols],
+                    rhs=words[group][:, k, :].bitcast(E2M1),
+                    rhs_scale=scales_w[GROUP * group + k],
+                    start=True,
+                    stop=True,
+                )
+                banks.append(acc)
+            return banks
+
+        def gate_all(group, banks, pieces):
+            experts = [GROUP * group + k for k in range(GROUP)]
+            for e in experts:
+                gated[e] = held.tile([P, N], F32, name=f"gated{e}")
+            for piece in range(pieces):
+                cols = slice(piece * N // pieces, (piece + 1) * N // pieces)
+                for k, e in enumerate(experts):
+                    nc.scalar.activation(gated[e][:, cols], banks[k][:, cols], COPY, scale=gate_cols[:, e : e + 1])
+
+        def turn(experts, i, tag):
+            width = len(experts) * C
+            turned = psum.tile([P, N], F32, name="turned", bufs=4)
+            for k, e in enumerate(experts):
+                nc.tensor.transpose(turned[:, k * C : (k + 1) * C], gated[e][:, i * P : (i + 1) * P], ident[:])
+            if tag is None:
+                slots = held.tile([P, width], F32, name=f"slots{experts[0]}_{i}")
+            else:
+                slots = held.tile([P, width], F32, name=f"slots{experts[0]}_{i}", tag=tag, align_bytes=64)
+            nc.scalar.copy(slots[:], turned[:, 0:width])
+            return slots
+
+        def direct(group, codes, scales, i, tag):
+            acc = psum.tile([P, N], F32, name="acc", bufs=4)
+            for k in range(GROUP):
+                cols = slice(k * C, (k + 1) * C)
+                nc.tensor.matmul_mx(
+                    out=acc[:, cols],
+                    lhsT=words[group][:, k, 2 * i * P : 2 * (i + 1) * P].bitcast(E2M1),
+                    lhsT_scale=scales_w[GROUP * group + k][:, i * P : (i + 1) * P],
+                    rhs=codes[:, cols].bitcast(E4M3),
+                    rhs_scale=scales[:, cols],
+                    start=True,
+                    stop=True,
+                )
+            if tag is None:
+                slots = held.tile([P, SPAN], F32, name=f"direct{group}_{i}")
+            else:
+                slots = held.tile([P, SPAN], F32, name=f"direct{group}_{i}", tag=tag, align_bytes=64)
+            nc.scalar.copy(slots[:], acc[:, 0:SPAN])
+            return slots
+
+        def scatter_gated(group, slots, i):
+            nc.vector.tensor_tensor(
+                windows[i][:].indirect(listed(group)), slots[:], gate_wide[:, group * SPAN : (group + 1) * SPAN], MULT
+            )
+
+        def scatter(group, count, slots, i):
+            nc.vector.tensor_copy(windows[i][:].indirect(listed(group, count)), slots[:])
+
+        for t0, width, chunk in raw:
+            half = width // 2
+            nc.vector.tensor_copy(pairs[:, t0 : t0 + half, :], chunk[:, :, 0:half].rearrange("p j t -> p t j"))
+            nc.scalar.copy(pairs[:, t0 + half : t0 + width, :], chunk[:, :, half:width].rearrange("p j t -> p t j"))
+
+        first = held.tile([P, SPAN * 4], BF16, name="first", tag="outer", align_bytes=64)
+        second = held.tile([P, SPAN * 4], BF16, name="second", tag="inner", align_bytes=64)
+        plane0 = held.tile([P, T], BF16, name="plane0", align_bytes=64)
+        gather_pairs(0, 1, first[:])
+        gather_raw(0, first[:], 0)
+        gather_pairs(1, 1, second[:])
+        gather_raw(0, first[:], 1)
+        operands = [quantise(0, 1, first[:])]
+        nc.scalar.copy(plane0[:], late[0][:])
+        gather_plane(1, second[:], 0, plane0)
+
+        rest = held.tile([P, 2 * SPAN * 4], BF16, name="rest", tag="outer", align_bytes=64)
+        halves = [rest[:, 0 : SPAN * 4], rest[:, SPAN * 4 : 2 * SPAN * 4]]
+        gather_pairs(2, 2, rest[:])
+        back = [direct(0, *operands[0], i, None) for i in range(3)]
+        for i in range(3):
+            scatter_gated(0, back[i], i)
+        plane1 = held.tile([P, T], BF16, name="plane1", tag="early", align_bytes=64)
+        nc.scalar.copy(plane1[:], late[1][:])
+        gather_plane(1, second[:], 1, plane1)
+        operands.append(quantise(1, 1, second[:]))
+        back.append(direct(0, *operands[0], 3, "inner"))
+        gate_turned = psum.tile([P, N], F32, name="turned", bufs=4)
+        nc.tensor.transpose(gate_turned[:, 0:P], gate_rows[:], ident[:])
+        gate_cols = held.tile([P, E], F32, name="gate_cols")
+        nc.scalar.copy(gate_cols[:], gate_turned[:, 0:E])
+        scatter_gated(0, back[3], 3)
+        back = [direct(1, *operands[1], i, None) for i in range(2)]
+        scatter_gated(1, back[0], 0)
+        scatter_gated(1, back[1], 1)
+        for j, plane in enumerate((plane0, plane1)):
+            gather_plane(2, halves[0], j, plane)
+            gather_plane(3, halves[1], j, plane)
+        codes, scales = quantise(2, 2, rest[:])
+        for i in range(2, TILES):
+            back.append(direct(1, *operands[1], i, "outer" if i == 2 else None))
+        for half in range(2):
+            gate_all(2 + half, multiply(2 + half, codes, scales, half), 1)
+        for i in range(2, TILES):
+            scatter_gated(1, back[i], i)
+        for i in range(TILES):
+            scatter(2, 2, turn([4, 5, 6, 7], i, None), i)
+
+        for i in range(TILES):
+            total = held.tile([P, T], F32, name=f"total{i}")
+            if i < TILES - 1:
+                nc.gpsimd.tensor_tensor(total[:], windows[i][:], residual[i][:], ADD)
+                nc.sync.dma_start(out[i * P : (i + 1) * P, :], total[:])
+            else:
+                lines = []
+                for t0, width in PIECES:
+                    upright = psum.tile([P, N], F32, name="turned", bufs=4)
+                    for b in range(0, width, P):
+                        nc.tensor.transpose(upright[:, b : b + P], residual[i][:, t0 + b : t0 + b + P], ident[:])
+                    rows = held.tile([P, width], F32, name=f"rows{t0}")
+                    nc.scalar.copy(rows[:], upright[:, 0:width])
+                    lines.append(rows)
+                for (t0, width), rows in zip(PIECES, lines):
+                    bank = psum.tile([P, N], F32, name="turned", bufs=4)
+                    for b in range(0, width, P):
+                        nc.tensor.transpose(bank[:, b : b + P], rows[:, b : b + P], ident[:])
+                    for c in range(0, width, width // 2):
+                        cols = slice(t0 + c, t0 + c + width // 2)
+                        nc.vector.tensor_tensor(total[:, cols], windows[i][:, cols], bank[:, c : c + width // 2], ADD)
+                        nc.sync.dma_start(out[i * P : (i + 1) * P, cols], total[:, cols])
+                cols = slice(896, T)
+                nc.gpsimd.tensor_tensor(total[:, cols], windows[i][:, cols], residual[i][:, cols], ADD)
+                nc.sync.dma_start(out[i * P : (i + 1) * P, cols], total[:, cols])

@@ -24,7 +24,7 @@ TILES = N // P
 GROUP = 2
 SPAN = GROUP * C
 PIECES = [(0, 512), (512, 384)]
-CHUNKS = [(0, 640), (640, 640)]
+HALF = T // 2
 
 
 def tile_moe_res_lin_none_kernel(tc, xT, xr, w_words, w_scales, gate, offs, out):
@@ -34,20 +34,15 @@ def tile_moe_res_lin_none_kernel(tc, xT, xr, w_words, w_scales, gate, offs, out)
         psum = ctx.enter_context(tc.psum_pool(name="psum", bufs=4))
 
         offsets = held.tile([P, E * C // 16], U16, name="offsets")
-
         x_rows = xT.rearrange("(p j) t -> p j t", j=4)
-        raw = []
-        for t0, width in CHUNKS:
-            chunk = held.tile([P, 2, width], F32, name=f"raw_{t0}")
-            nc.sync.dma_start(chunk[:], x_rows[:, 0:2, t0 : t0 + width])
-            raw.append((t0, width, chunk))
-            if t0 == 0:
-                nc.sync.dma_start(offsets[:], offs)
         scale_rows = w_scales.rearrange("e a q n -> (e a) q n")
+        word_rows = w_words.rearrange("e a p b -> (e a) p b")
+        scales_w = {}
+        words = {}
 
         def load_scales(e0, count):
             rows = held.tile([P, count, N], U8, name=f"scales_w{e0}", align_bytes=64)
-            nc.gpsimd.memset(rows[:].rearrange("p e n -> p (e n)").bitcast(I32), 0)
+            (nc.vector if e0 == 0 else nc.gpsimd).memset(rows[:].rearrange("p e n -> p (e n)").bitcast(I32), 0)
             for quad in range(4):
                 nc.sync.dma_start(
                     rows[32 * quad : 32 * quad + 4].bitcast(I32),
@@ -56,188 +51,173 @@ def tile_moe_res_lin_none_kernel(tc, xT, xr, w_words, w_scales, gate, offs, out)
             for k in range(count):
                 scales_w[e0 + k] = rows[:, k, :]
 
-        scales_w = {}
-        load_scales(0, GROUP)
-        late = []
-        for j in range(2):
-            late_plane = held.tile([P, T], F32, name=f"late{j}")
-            nc.sync.dma_start(late_plane[:], x_rows[:, 2 + j, :])
-            late.append(late_plane)
-
-        ident = held.tile([P, P], F32, name="ident")
-        make_identity(nc, ident[:])
-        word_rows = w_words.rearrange("e a p b -> (e a) p b")
-        words = []
-        for e0 in range(0, E, GROUP):
-            group_words = held.tile([P, GROUP, 2 * N], U8, name=f"words{e0}", align_bytes=64)
+        def load_words(e0):
+            pair = held.tile([P, GROUP, 2 * N], U8, name=f"words{e0}", align_bytes=64)
             nc.sync.dma_start(
-                group_words[:].bitcast(I32),
-                word_rows[e0 : e0 + GROUP].bitcast(I32).rearrange("e p b -> p e b"),
+                pair[:].bitcast(I32), word_rows[e0 : e0 + GROUP].bitcast(I32).rearrange("e p b -> p e b")
             )
-            words.append(group_words)
-            if e0 == 0:
-                gate_wide = held.tile([P, 2 * SPAN], F32, name="gate_wide")
-                nc.sync.dma_start(gate_wide[:], gate[0:P, 0 : 2 * SPAN])
-                load_scales(GROUP, E - GROUP)
-                gate_rows = held.tile([P, P], F32, name="gate_rows")
-                nc.gpsimd.memset(gate_rows[:], 0.0)
-                nc.sync.dma_start(gate_rows[0:E, :], gate[0:1, :].rearrange("r (e c) -> (r e) c", e=E))
+            for k in range(GROUP):
+                words[e0 + k] = pair[:, k, :]
+
+        raw = [held.tile([P, T], F32, name=f"raw{j}") for j in range(4)]
+        nc.sync.dma_start(raw[0][:, 0:HALF], x_rows[:, 0, 0:HALF])
+        nc.sync.dma_start(raw[0][:, HALF:T], x_rows[:, 0, HALF:T])
+        nc.sync.dma_start(offsets[:], offs)
+        nc.sync.dma_start(raw[1][:], x_rows[:, 1, :])
+        nc.sync.dma_start(raw[2][:], x_rows[:, 2, :])
+        load_scales(0, GROUP)
+        nc.sync.dma_start(raw[3][:], x_rows[:, 3, :])
+        load_words(0)
+        gate_wide = held.tile([P, 2 * SPAN], F32, name="gate_wide")
+        nc.sync.dma_start(gate_wide[:], gate[0:P, 0 : 2 * SPAN])
+        load_words(2)
+        load_scales(GROUP, E - GROUP)
+        gate_rows = held.tile([P, P], F32, name="gate_rows")
+        nc.gpsimd.memset(gate_rows[:], 0.0)
+        nc.sync.dma_start(gate_rows[0:E, :], gate[0:1, :].rearrange("r (e c) -> (r e) c", e=E))
+        load_words(4)
+        load_words(6)
         residual = []
         for i in range(TILES):
             xr_tile = held.tile([P, T], F32, name=f"xr{i}")
             nc.sync.dma_start(xr_tile[:], xr[i * P : (i + 1) * P, :])
             residual.append(xr_tile)
 
+        ident = held.tile([P, P], F32, name="ident")
+        make_identity(nc, ident[:])
         windows = []
         for i in range(TILES):
             window = held.tile([P, T], F32, name=f"window{i}")
-            (nc.vector if i < 2 else nc.gpsimd).memset(window[:], 0.0)
+            if i < 2:
+                nc.vector.memset(window[:], 0.0)
+            elif i == 2:
+                nc.gpsimd.memset(window[:], 0.0)
+            else:
+                nc.scalar.copy(window[:], windows[0][:])
             windows.append(window)
 
-        pairs = held.tile([P, T, 2], BF16, name="pairs", align_bytes=64)
-        gated = {}
+        def listed(s0, count):
+            return offsets[:, s0 // 16 : (s0 + count) // 16]
 
-        def listed(group, count=1):
-            return offsets[:, group * SPAN // 16 : (group + count) * SPAN // 16]
+        def lane(target, j):
+            return target[:].rearrange("p (s j) -> p s j", j=4)[:, :, j]
 
-        def gather_pairs(group, count, target):
-            window = pairs[:].rearrange("p t j -> p (t j)").bitcast(U32)
-            slots = target.bitcast(U32).rearrange("p (s u) -> p s u", u=2)
-            nc.vector.tensor_copy(slots[:, :, 0], window.indirect(listed(group, count)))
-
-        def gather_raw(group, target, j):
-            slots = target.rearrange("p (s j) -> p s j", j=4)[:, :, 2 + j]
-            nc.vector.tensor_copy(slots, late[j][:].indirect(listed(group)))
-
-        def gather_plane(group, target, j, plane):
-            slots = target.rearrange("p (s j) -> p s j", j=4)[:, :, 2 + j]
-            nc.scalar.activation(slots, plane[:].indirect(listed(group)), COPY)
-
-        def quantise(group, count, source):
-            codes = held.tile([P, count * SPAN], U32, name=f"codes{group}", tag="early" if group == 0 else f"codes{group}", align_bytes=64)
-            scales = held.tile([P, count * SPAN], U8, name=f"scales{group}", align_bytes=64)
-            nc.vector.quantize_mx(out=codes[:].bitcast(E4M3), scales=scales[:], in_=source)
+        def quantise(name, source, count, tag):
+            codes = held.tile([P, count], U32, name=f"codes_{name}", tag=tag, align_bytes=64)
+            scales = held.tile([P, count], U8, name=f"scales_{name}", align_bytes=64)
+            nc.vector.quantize_mx(out=codes[:].bitcast(E4M3), scales=scales[:], in_=source[:])
             return codes, scales
 
-        def multiply(group, codes, scales, place):
-            banks = []
-            for k in range(GROUP):
-                cols = slice((GROUP * place + k) * C, (GROUP * place + k + 1) * C)
-                acc = psum.tile([P, N], F32, name="acc", bufs=4)
-                nc.tensor.matmul_mx(
-                    out=acc[:],
-                    lhsT=codes[:, cols].bitcast(E4M3),
-                    lhsT_scale=scales[:, cols],
-                    rhs=words[group][:, k, :].bitcast(E2M1),
-                    rhs_scale=scales_w[GROUP * group + k],
-                    start=True,
-                    stop=True,
-                )
-                banks.append(acc)
-            return banks
+        tokens = {}
 
-        def gate_all(group, banks, pieces):
-            experts = [GROUP * group + k for k in range(GROUP)]
-            for e in experts:
-                gated[e] = held.tile([P, N], F32, name=f"gated{e}")
-            for piece in range(pieces):
-                cols = slice(piece * N // pieces, (piece + 1) * N // pieces)
-                for k, e in enumerate(experts):
-                    nc.scalar.activation(gated[e][:, cols], banks[k][:, cols], COPY, scale=gate_cols[:, e : e + 1])
+        def deal(e0, count, codes, scales):
+            for k in range(count):
+                tokens[e0 + k] = (codes[:, k * C : (k + 1) * C].bitcast(E4M3), scales[:, k * C : (k + 1) * C])
 
-        def turn(experts, i, tag):
-            width = len(experts) * C
-            turned = psum.tile([P, N], F32, name="turned", bufs=4)
-            for k, e in enumerate(experts):
-                nc.tensor.transpose(turned[:, k * C : (k + 1) * C], gated[e][:, i * P : (i + 1) * P], ident[:])
-            if tag is None:
-                slots = held.tile([P, width], F32, name=f"slots{experts[0]}_{i}")
-            else:
-                slots = held.tile([P, width], F32, name=f"slots{experts[0]}_{i}", tag=tag, align_bytes=64)
-            nc.scalar.copy(slots[:], turned[:, 0:width])
-            return slots
-
-        def direct(group, codes, scales, i, tag):
+        def direct(e0, i, tag):
             acc = psum.tile([P, N], F32, name="acc", bufs=4)
             for k in range(GROUP):
-                cols = slice(k * C, (k + 1) * C)
                 nc.tensor.matmul_mx(
-                    out=acc[:, cols],
-                    lhsT=words[group][:, k, 2 * i * P : 2 * (i + 1) * P].bitcast(E2M1),
-                    lhsT_scale=scales_w[GROUP * group + k][:, i * P : (i + 1) * P],
-                    rhs=codes[:, cols].bitcast(E4M3),
-                    rhs_scale=scales[:, cols],
+                    out=acc[:, k * C : (k + 1) * C],
+                    lhsT=words[e0 + k][:, 2 * i * P : 2 * (i + 1) * P].bitcast(E2M1),
+                    lhsT_scale=scales_w[e0 + k][:, i * P : (i + 1) * P],
+                    rhs=tokens[e0 + k][0],
+                    rhs_scale=tokens[e0 + k][1],
                     start=True,
                     stop=True,
                 )
-            if tag is None:
-                slots = held.tile([P, SPAN], F32, name=f"direct{group}_{i}")
-            else:
-                slots = held.tile([P, SPAN], F32, name=f"direct{group}_{i}", tag=tag, align_bytes=64)
+            slots = held.tile([P, SPAN], F32, name=f"direct{e0}_{i}", tag=tag, align_bytes=64)
             nc.scalar.copy(slots[:], acc[:, 0:SPAN])
             return slots
 
-        def scatter_gated(group, slots, i):
+        def scatter_gated(e0, slots, i):
             nc.vector.tensor_tensor(
-                windows[i][:].indirect(listed(group)), slots[:], gate_wide[:, group * SPAN : (group + 1) * SPAN], MULT
+                windows[i][:].indirect(listed(e0 * C, SPAN)), slots[:], gate_wide[:, e0 * C : e0 * C + SPAN], MULT
             )
 
-        def scatter(group, count, slots, i):
-            nc.vector.tensor_copy(windows[i][:].indirect(listed(group, count)), slots[:])
+        gated = {}
 
-        for t0, width, chunk in raw:
-            half = width // 2
-            nc.vector.tensor_copy(pairs[:, t0 : t0 + half, :], chunk[:, :, 0:half].rearrange("p j t -> p t j"))
-            nc.scalar.copy(pairs[:, t0 + half : t0 + width, :], chunk[:, :, half:width].rearrange("p j t -> p t j"))
+        def by_slot(experts, n0, width):
+            acc = psum.tile([P, N], F32, name="acc", bufs=4)
+            for k, e in enumerate(experts):
+                nc.tensor.matmul_mx(
+                    out=acc[:, k * width : (k + 1) * width],
+                    lhsT=tokens[e][0],
+                    lhsT_scale=tokens[e][1],
+                    rhs=words[e][:, 2 * n0 : 2 * (n0 + width)].bitcast(E2M1),
+                    rhs_scale=scales_w[e][:, n0 : n0 + width],
+                    start=True,
+                    stop=True,
+                )
+            for k, e in enumerate(experts):
+                rows = held.tile([P, width], F32, name=f"gated{e}")
+                nc.scalar.activation(rows[:], acc[:, k * width : (k + 1) * width], COPY, scale=gate_cols[:, e : e + 1])
+                gated[e] = (rows, n0)
 
-        first = held.tile([P, SPAN * 4], BF16, name="first", tag="outer", align_bytes=64)
-        second = held.tile([P, SPAN * 4], BF16, name="second", tag="inner", align_bytes=64)
-        plane0 = held.tile([P, T], BF16, name="plane0", align_bytes=64)
-        gather_pairs(0, 1, first[:])
-        gather_raw(0, first[:], 0)
-        gather_pairs(1, 1, second[:])
-        gather_raw(0, first[:], 1)
-        operands = [quantise(0, 1, first[:])]
-        nc.scalar.copy(plane0[:], late[0][:])
-        gather_plane(1, second[:], 0, plane0)
+        def turn(experts, i, slots):
+            turned = psum.tile([P, N], F32, name="turned", bufs=4)
+            for k, e in enumerate(experts):
+                rows, n0 = gated[e]
+                nc.tensor.transpose(turned[:, k * C : (k + 1) * C], rows[:, i * P - n0 : (i + 1) * P - n0], ident[:])
+            nc.scalar.copy(slots, turned[:, 0 : len(experts) * C])
 
-        rest = held.tile([P, 2 * SPAN * 4], BF16, name="rest", tag="outer", align_bytes=64)
-        halves = [rest[:, 0 : SPAN * 4], rest[:, SPAN * 4 : 2 * SPAN * 4]]
-        gather_pairs(2, 2, rest[:])
-        back = [direct(0, *operands[0], i, None) for i in range(3)]
-        for i in range(3):
-            scatter_gated(0, back[i], i)
-        plane1 = held.tile([P, T], BF16, name="plane1", tag="early", align_bytes=64)
-        nc.scalar.copy(plane1[:], late[1][:])
-        gather_plane(1, second[:], 1, plane1)
-        operands.append(quantise(1, 1, second[:]))
-        back.append(direct(0, *operands[0], 3, "inner"))
+        first = held.tile([P, SPAN * 4], BF16, name="first", tag="first", align_bytes=64)
+        mid = held.tile([P, 2 * SPAN * 4], BF16, name="mid", align_bytes=64)
+        planes = []
+        for j in range(3):
+            plane = held.tile([P, T], BF16, name=f"plane{j}", align_bytes=64)
+            if j == 0:
+                nc.vector.tensor_copy(plane[:, 0:HALF], raw[0][:, 0:HALF])
+                nc.scalar.copy(plane[:, HALF:T], raw[0][:, HALF:T])
+            else:
+                nc.vector.tensor_copy(plane[:], raw[j][:])
+            nc.vector.tensor_copy(lane(first, j), raw[j][:].indirect(listed(0, SPAN)))
+            nc.scalar.activation(lane(mid, j), plane[:].indirect(listed(SPAN, 2 * SPAN)), COPY)
+            planes.append(plane)
+        nc.vector.tensor_copy(lane(first, 3), raw[3][:].indirect(listed(0, SPAN)))
+        deal(0, GROUP, *quantise("first", first, SPAN, "codes0"))
+        plane = held.tile([P, T], BF16, name="plane3", tag="first", align_bytes=64)
+        nc.vector.tensor_copy(plane[:], raw[3][:])
+        planes.append(plane)
+
+        back = [direct(0, i, f"back{i}") for i in range(2)]
+        nc.scalar.activation(lane(mid, 3), planes[3][:].indirect(listed(SPAN, 2 * SPAN)), COPY)
+        back.extend(direct(0, i, f"back{i}") for i in range(2, TILES))
+        scatter_gated(0, back[0], 0)
+        deal(2, 2 * GROUP, *quantise("mid", mid, 2 * SPAN, "back0"))
+        scatter_gated(0, back[1], 1)
+        scatter_gated(0, back[2], 2)
+        last = held.tile([P, SPAN * 4], BF16, name="last", tag="codes0", align_bytes=64)
+        for j in range(4):
+            nc.scalar.activation(lane(last, j), planes[j][:].indirect(listed(3 * SPAN, SPAN)), COPY)
+        deal(6, GROUP, *quantise("last", last, SPAN, "back2"))
+        scatter_gated(0, back[3], 3)
+
+        back = [direct(2, i, f"next{i}") for i in range(TILES - 1)]
         gate_turned = psum.tile([P, N], F32, name="turned", bufs=4)
         nc.tensor.transpose(gate_turned[:, 0:P], gate_rows[:], ident[:])
         gate_cols = held.tile([P, E], F32, name="gate_cols")
         nc.scalar.copy(gate_cols[:], gate_turned[:, 0:E])
-        scatter_gated(0, back[3], 3)
-        back = [direct(1, *operands[1], i, None) for i in range(2)]
-        scatter_gated(1, back[0], 0)
-        scatter_gated(1, back[1], 1)
-        for j, plane in enumerate((plane0, plane1)):
-            gather_plane(2, halves[0], j, plane)
-            gather_plane(3, halves[1], j, plane)
-        codes, scales = quantise(2, 2, rest[:])
-        for i in range(2, TILES):
-            back.append(direct(1, *operands[1], i, "outer" if i == 2 else None))
-        for half in range(2):
-            gate_all(2 + half, multiply(2 + half, codes, scales, half), 1)
-        for i in range(2, TILES):
-            scatter_gated(1, back[i], i)
+        for i in range(TILES - 1):
+            scatter_gated(2, back[i], i)
+        for e in range(4, E):
+            by_slot([e], 0, N)
+        by_slot([2, 3], (TILES - 1) * P, P)
         for i in range(TILES):
-            scatter(2, 2, turn([4, 5, 6, 7], i, None), i)
+            s0 = 2 * SPAN if i < TILES - 1 else SPAN
+            slots = held.tile([P, E * C - s0], F32, name=f"slots{i}")
+            turn([4, 5, 6, 7], i, slots[:, 2 * SPAN - s0 :])
+            if i == TILES - 1:
+                turn([2, 3], i, slots[:, 0:SPAN])
+            nc.vector.tensor_copy(windows[i][:].indirect(listed(s0, E * C - s0)), slots[:])
 
         for i in range(TILES):
             total = held.tile([P, T], F32, name=f"total{i}")
             if i < TILES - 1:
-                nc.gpsimd.tensor_tensor(total[:], windows[i][:], residual[i][:], ADD)
-                nc.sync.dma_start(out[i * P : (i + 1) * P, :], total[:])
+                for t0 in range(0, T, HALF):
+                    cols = slice(t0, t0 + HALF)
+                    nc.gpsimd.tensor_tensor(total[:, cols], windows[i][:, cols], residual[i][:, cols], ADD)
+                    nc.sync.dma_start(out[i * P : (i + 1) * P, cols], total[:, cols])
             else:
                 lines = []
                 for t0, width in PIECES:

@@ -59,11 +59,12 @@ def tile_moe_res_lin_none_kernel(tc, xT, xr, w_words, w_scales, gate, offs, out)
             for k in range(GROUP):
                 words[e0 + k] = pair[:, k, :]
 
-        raw = [held.tile([P, T], F32, name=f"raw{j}") for j in range(4)]
+        raw = [held.tile([P, T], F32, name=f"raw{j}", tag=f"raw{j}", align_bytes=64) for j in range(4)]
         nc.sync.dma_start(raw[0][:, 0:HALF], x_rows[:, 0, 0:HALF])
         nc.sync.dma_start(raw[0][:, HALF:T], x_rows[:, 0, HALF:T])
         nc.sync.dma_start(offsets[:], offs)
-        nc.sync.dma_start(raw[1][:], x_rows[:, 1, :])
+        nc.sync.dma_start(raw[1][:, 0:HALF], x_rows[:, 1, 0:HALF])
+        nc.sync.dma_start(raw[1][:, HALF:T], x_rows[:, 1, HALF:T])
         nc.sync.dma_start(raw[2][:], x_rows[:, 2, :])
         load_scales(0, GROUP)
         nc.sync.dma_start(raw[3][:], x_rows[:, 3, :])
@@ -85,16 +86,13 @@ def tile_moe_res_lin_none_kernel(tc, xT, xr, w_words, w_scales, gate, offs, out)
 
         ident = held.tile([P, P], F32, name="ident")
         make_identity(nc, ident[:])
-        windows = []
-        for i in range(TILES):
-            window = held.tile([P, T], F32, name=f"window{i}")
+        windows = {}
+        for i in (0, 1, 3):
+            windows[i] = held.tile([P, T], F32, name=f"window{i}")
             if i < 2:
-                nc.vector.memset(window[:], 0.0)
-            elif i == 2:
-                nc.gpsimd.memset(window[:], 0.0)
+                nc.vector.memset(windows[i][:], 0.0)
             else:
-                nc.scalar.copy(window[:], windows[0][:])
-            windows.append(window)
+                nc.scalar.copy(windows[i][:], windows[0][:])
 
         def listed(s0, count):
             return offsets[:, s0 // 16 : (s0 + count) // 16]
@@ -102,10 +100,15 @@ def tile_moe_res_lin_none_kernel(tc, xT, xr, w_words, w_scales, gate, offs, out)
         def lane(target, j):
             return target[:].rearrange("p (s j) -> p s j", j=4)[:, :, j]
 
-        def quantise(name, source, count, tag):
+        def quantise(name, source, count, tag, step):
             codes = held.tile([P, count], U32, name=f"codes_{name}", tag=tag, align_bytes=64)
-            scales = held.tile([P, count], U8, name=f"scales_{name}", align_bytes=64)
-            nc.vector.quantize_mx(out=codes[:].bitcast(E4M3), scales=scales[:], in_=source[:])
+            scales = held.tile([P, count], U8, name=f"scales_{name}", tag=f"scales_{name}", align_bytes=64)
+            for s0 in range(0, count, step):
+                nc.vector.quantize_mx(
+                    out=codes[:, s0 : s0 + step].bitcast(E4M3),
+                    scales=scales[:, s0 : s0 + step],
+                    in_=source[:, 4 * s0 : 4 * (s0 + step)],
+                )
             return codes, scales
 
         tokens = {}
@@ -114,20 +117,21 @@ def tile_moe_res_lin_none_kernel(tc, xT, xr, w_words, w_scales, gate, offs, out)
             for k in range(count):
                 tokens[e0 + k] = (codes[:, k * C : (k + 1) * C].bitcast(E4M3), scales[:, k * C : (k + 1) * C])
 
-        def direct(e0, i, tag):
-            acc = psum.tile([P, N], F32, name="acc", bufs=4)
-            for k in range(GROUP):
-                nc.tensor.matmul_mx(
-                    out=acc[:, k * C : (k + 1) * C],
-                    lhsT=words[e0 + k][:, 2 * i * P : 2 * (i + 1) * P].bitcast(E2M1),
-                    lhsT_scale=scales_w[e0 + k][:, i * P : (i + 1) * P],
-                    rhs=tokens[e0 + k][0],
-                    rhs_scale=tokens[e0 + k][1],
-                    start=True,
-                    stop=True,
-                )
+        def direct(e0, i, tag, step=GROUP):
             slots = held.tile([P, SPAN], F32, name=f"direct{e0}_{i}", tag=tag, align_bytes=64)
-            nc.scalar.copy(slots[:], acc[:, 0:SPAN])
+            for k0 in range(0, GROUP, step):
+                acc = psum.tile([P, N], F32, name="acc", bufs=4)
+                for k in range(step):
+                    nc.tensor.matmul_mx(
+                        out=acc[:, k * C : (k + 1) * C],
+                        lhsT=words[e0 + k0 + k][:, 2 * i * P : 2 * (i + 1) * P].bitcast(E2M1),
+                        lhsT_scale=scales_w[e0 + k0 + k][:, i * P : (i + 1) * P],
+                        rhs=tokens[e0 + k0 + k][0],
+                        rhs_scale=tokens[e0 + k0 + k][1],
+                        start=True,
+                        stop=True,
+                    )
+                nc.scalar.copy(slots[:, k0 * C : (k0 + step) * C], acc[:, 0 : step * C])
             return slots
 
         def scatter_gated(e0, slots, i):
@@ -165,35 +169,37 @@ def tile_moe_res_lin_none_kernel(tc, xT, xr, w_words, w_scales, gate, offs, out)
         mid = held.tile([P, 2 * SPAN * 4], BF16, name="mid", align_bytes=64)
         planes = []
         for j in range(3):
-            plane = held.tile([P, T], BF16, name=f"plane{j}", align_bytes=64)
-            if j == 0:
-                nc.vector.tensor_copy(plane[:, 0:HALF], raw[0][:, 0:HALF])
-                nc.scalar.copy(plane[:, HALF:T], raw[0][:, HALF:T])
+            plane = held.tile([P, T], BF16, name=f"plane{j}", tag=f"plane{j}", align_bytes=64)
+            if j < 2:
+                nc.vector.tensor_copy(plane[:, 0:HALF], raw[j][:, 0:HALF])
+                nc.vector.tensor_copy(plane[:, HALF:T], raw[j][:, HALF:T])
             else:
                 nc.vector.tensor_copy(plane[:], raw[j][:])
             nc.vector.tensor_copy(lane(first, j), raw[j][:].indirect(listed(0, SPAN)))
             nc.scalar.activation(lane(mid, j), plane[:].indirect(listed(SPAN, 2 * SPAN)), COPY)
             planes.append(plane)
         nc.vector.tensor_copy(lane(first, 3), raw[3][:].indirect(listed(0, SPAN)))
-        deal(0, GROUP, *quantise("first", first, SPAN, "codes0"))
+        deal(0, GROUP, *quantise("first", first, SPAN, "codes0", C))
         plane = held.tile([P, T], BF16, name="plane3", tag="first", align_bytes=64)
         nc.vector.tensor_copy(plane[:], raw[3][:])
         planes.append(plane)
 
-        back = [direct(0, i, f"back{i}") for i in range(2)]
+        back = [direct(0, 0, "back0", 1), direct(0, 1, "back1")]
         nc.scalar.activation(lane(mid, 3), planes[3][:].indirect(listed(SPAN, 2 * SPAN)), COPY)
-        back.extend(direct(0, i, f"back{i}") for i in range(2, TILES))
+        back.extend([direct(0, 2, "raw3"), direct(0, 3, "back3")])
+        windows[2] = held.tile([P, T], F32, name="window2", tag="scales_first", align_bytes=64)
+        nc.gpsimd.memset(windows[2][:], 0.0)
         scatter_gated(0, back[0], 0)
-        deal(2, 2 * GROUP, *quantise("mid", mid, 2 * SPAN, "back0"))
+        deal(2, 2 * GROUP, *quantise("mid", mid, 2 * SPAN, "back0", 2 * SPAN))
         scatter_gated(0, back[1], 1)
         scatter_gated(0, back[2], 2)
         last = held.tile([P, SPAN * 4], BF16, name="last", tag="codes0", align_bytes=64)
         for j in range(4):
             nc.scalar.activation(lane(last, j), planes[j][:].indirect(listed(3 * SPAN, SPAN)), COPY)
-        deal(6, GROUP, *quantise("last", last, SPAN, "back2"))
+        deal(6, GROUP, *quantise("last", last, SPAN, "codes3", SPAN))
         scatter_gated(0, back[3], 3)
 
-        back = [direct(2, i, f"next{i}") for i in range(TILES - 1)]
+        back = [direct(2, i, f"plane{2 - i}") for i in range(TILES - 1)]
         gate_turned = psum.tile([P, N], F32, name="turned", bufs=4)
         nc.tensor.transpose(gate_turned[:, 0:P], gate_rows[:], ident[:])
         gate_cols = held.tile([P, E], F32, name="gate_cols")

@@ -20,29 +20,33 @@ COPY = mybir.ActivationFunctionType.Copy
 ADD = mybir.AluOpType.add
 MULT = mybir.AluOpType.mult
 
+PACK = 4
 TILES = N // P
+LAST = TILES - 1
 GROUP = 2
 SPAN = GROUP * C
-PIECES = [(0, 512), (512, 384)]
 HALF = T // 2
+BANKS = 4
+PIECES = [(0, 512), (512, 384)]
+SHARED = 896
 
 
 def tile_moe_res_lin_none_kernel(tc, xT, xr, w_words, w_scales, gate, offs, out):
     nc = tc.nc
     with ExitStack() as ctx:
         held = ctx.enter_context(tc.tile_pool(name="held", bufs=1))
-        psum = ctx.enter_context(tc.psum_pool(name="psum", bufs=4))
+        psum = ctx.enter_context(tc.psum_pool(name="psum", bufs=BANKS))
 
         offsets = held.tile([P, E * C // 16], U16, name="offsets")
-        x_rows = xT.rearrange("(p j) t -> p j t", j=4)
+        x_rows = xT.rearrange("(p j) t -> p j t", j=PACK)
         scale_rows = w_scales.rearrange("e a q n -> (e a) q n")
         word_rows = w_words.rearrange("e a p b -> (e a) p b")
         scales_w = {}
         words = {}
 
-        def load_scales(e0, count):
+        def load_scales(e0, count, engine):
             rows = held.tile([P, count, N], U8, name=f"scales_w{e0}", align_bytes=64)
-            (nc.vector if e0 == 0 else nc.gpsimd).memset(rows[:].rearrange("p e n -> p (e n)").bitcast(I32), 0)
+            engine.memset(rows[:].rearrange("p e n -> p (e n)").bitcast(I32), 0)
             for quad in range(4):
                 nc.sync.dma_start(
                     rows[32 * quad : 32 * quad + 4].bitcast(I32),
@@ -59,23 +63,25 @@ def tile_moe_res_lin_none_kernel(tc, xT, xr, w_words, w_scales, gate, offs, out)
             for k in range(GROUP):
                 words[e0 + k] = pair[:, k, :]
 
-        raw = [held.tile([P, T], F32, name=f"raw{j}", tag=f"raw{j}", align_bytes=64) for j in range(4)]
-        nc.sync.dma_start(raw[0][:, 0:HALF], x_rows[:, 0, 0:HALF])
-        nc.sync.dma_start(raw[0][:, HALF:T], x_rows[:, 0, HALF:T])
-        nc.sync.dma_start(offsets[:], offs)
-        nc.sync.dma_start(raw[1][:, 0:HALF], x_rows[:, 1, 0:HALF])
-        nc.sync.dma_start(raw[1][:, HALF:T], x_rows[:, 1, HALF:T])
+        raw = [held.tile([P, T], F32, name=f"raw{j}", tag=f"raw{j}", align_bytes=64) for j in range(PACK)]
+        for j in range(2):
+            nc.sync.dma_start(raw[j][:, 0:HALF], x_rows[:, j, 0:HALF])
+            nc.sync.dma_start(raw[j][:, HALF:T], x_rows[:, j, HALF:T])
+            if j == 0:
+                nc.sync.dma_start(offsets[:], offs)
         nc.sync.dma_start(raw[2][:], x_rows[:, 2, :])
-        load_scales(0, GROUP)
+        load_scales(0, GROUP, nc.vector)
         nc.sync.dma_start(raw[3][:], x_rows[:, 3, :])
         load_words(0)
         gate_wide = held.tile([P, 2 * SPAN], F32, name="gate_wide")
         nc.sync.dma_start(gate_wide[:], gate[0:P, 0 : 2 * SPAN])
         load_words(2)
-        load_scales(GROUP, E - GROUP)
+        load_scales(GROUP, E - GROUP, nc.gpsimd)
         gate_rows = held.tile([P, P], F32, name="gate_rows")
         nc.gpsimd.memset(gate_rows[:], 0.0)
-        nc.sync.dma_start(gate_rows[0:E, :], gate[0:1, :].rearrange("r (e c) -> (r e) c", e=E))
+        by_expert = gate[0:1, :].rearrange("r (e c) -> (r e) c", e=E)
+        nc.sync.dma_start(gate_rows[4:E, :], by_expert[4:E])
+        nc.sync.dma_start(gate_rows[2:4, :], by_expert[2:4])
         load_words(4)
         load_words(6)
         residual = []
@@ -86,48 +92,44 @@ def tile_moe_res_lin_none_kernel(tc, xT, xr, w_words, w_scales, gate, offs, out)
 
         ident = held.tile([P, P], F32, name="ident")
         make_identity(nc, ident[:])
-        windows = {}
-        for i in (0, 1, 3):
-            windows[i] = held.tile([P, T], F32, name=f"window{i}")
-            if i < 2:
-                nc.vector.memset(windows[i][:], 0.0)
-            else:
-                nc.scalar.copy(windows[i][:], windows[0][:])
+        windows = {i: held.tile([P, T], F32, name=f"window{i}") for i in (0, 1, LAST)}
+        nc.vector.memset(windows[0][:], 0.0)
+        nc.vector.memset(windows[1][:], 0.0)
+        nc.scalar.copy(windows[LAST][:], windows[0][:])
 
         def listed(s0, count):
             return offsets[:, s0 // 16 : (s0 + count) // 16]
 
         def lane(target, j):
-            return target[:].rearrange("p (s j) -> p s j", j=4)[:, :, j]
-
-        def quantise(name, source, count, tag, step):
-            codes = held.tile([P, count], U32, name=f"codes_{name}", tag=tag, align_bytes=64)
-            scales = held.tile([P, count], U8, name=f"scales_{name}", tag=f"scales_{name}", align_bytes=64)
-            for s0 in range(0, count, step):
-                nc.vector.quantize_mx(
-                    out=codes[:, s0 : s0 + step].bitcast(E4M3),
-                    scales=scales[:, s0 : s0 + step],
-                    in_=source[:, 4 * s0 : 4 * (s0 + step)],
-                )
-            return codes, scales
+            return target[:].rearrange("p (s j) -> p s j", j=PACK)[:, :, j]
 
         tokens = {}
 
-        def deal(e0, count, codes, scales):
+        def quantise(name, source, e0, count, tag, step):
+            width = count * C
+            codes = held.tile([P, width], U32, name=f"codes_{name}", tag=tag, align_bytes=64)
+            scales = held.tile([P, width], U8, name=f"scales_{name}", tag=f"scales_{name}", align_bytes=64)
+            for s0 in range(0, width, step):
+                nc.vector.quantize_mx(
+                    out=codes[:, s0 : s0 + step].bitcast(E4M3),
+                    scales=scales[:, s0 : s0 + step],
+                    in_=source[:, PACK * s0 : PACK * (s0 + step)],
+                )
             for k in range(count):
                 tokens[e0 + k] = (codes[:, k * C : (k + 1) * C].bitcast(E4M3), scales[:, k * C : (k + 1) * C])
 
         def direct(e0, i, tag, step=GROUP):
             slots = held.tile([P, SPAN], F32, name=f"direct{e0}_{i}", tag=tag, align_bytes=64)
             for k0 in range(0, GROUP, step):
-                acc = psum.tile([P, N], F32, name="acc", bufs=4)
+                acc = psum.tile([P, N], F32, name="acc", bufs=BANKS)
                 for k in range(step):
+                    e = e0 + k0 + k
                     nc.tensor.matmul_mx(
                         out=acc[:, k * C : (k + 1) * C],
-                        lhsT=words[e0 + k0 + k][:, 2 * i * P : 2 * (i + 1) * P].bitcast(E2M1),
-                        lhsT_scale=scales_w[e0 + k0 + k][:, i * P : (i + 1) * P],
-                        rhs=tokens[e0 + k0 + k][0],
-                        rhs_scale=tokens[e0 + k0 + k][1],
+                        lhsT=words[e][:, 2 * i * P : 2 * (i + 1) * P].bitcast(E2M1),
+                        lhsT_scale=scales_w[e][:, i * P : (i + 1) * P],
+                        rhs=tokens[e][0],
+                        rhs_scale=tokens[e][1],
                         start=True,
                         stop=True,
                     )
@@ -142,7 +144,7 @@ def tile_moe_res_lin_none_kernel(tc, xT, xr, w_words, w_scales, gate, offs, out)
         gated = {}
 
         def by_slot(experts, n0, width):
-            acc = psum.tile([P, N], F32, name="acc", bufs=4)
+            acc = psum.tile([P, N], F32, name="acc", bufs=BANKS)
             for k, e in enumerate(experts):
                 nc.tensor.matmul_mx(
                     out=acc[:, k * width : (k + 1) * width],
@@ -158,17 +160,17 @@ def tile_moe_res_lin_none_kernel(tc, xT, xr, w_words, w_scales, gate, offs, out)
                 nc.scalar.activation(rows[:], acc[:, k * width : (k + 1) * width], COPY, scale=gate_cols[:, e : e + 1])
                 gated[e] = (rows, n0)
 
-        def turn(experts, i, slots):
-            turned = psum.tile([P, N], F32, name="turned", bufs=4)
+        def turn(experts, i, target):
+            turned = psum.tile([P, N], F32, name="turned", bufs=BANKS)
             for k, e in enumerate(experts):
                 rows, n0 = gated[e]
                 nc.tensor.transpose(turned[:, k * C : (k + 1) * C], rows[:, i * P - n0 : (i + 1) * P - n0], ident[:])
-            nc.scalar.copy(slots, turned[:, 0 : len(experts) * C])
+            nc.scalar.copy(target, turned[:, 0 : len(experts) * C])
 
-        first = held.tile([P, SPAN * 4], BF16, name="first", tag="first", align_bytes=64)
-        mid = held.tile([P, 2 * SPAN * 4], BF16, name="mid", align_bytes=64)
+        first = held.tile([P, SPAN * PACK], BF16, name="first", tag="first", align_bytes=64)
+        mid = held.tile([P, 2 * SPAN * PACK], BF16, name="mid", align_bytes=64)
         planes = []
-        for j in range(3):
+        for j in range(PACK - 1):
             plane = held.tile([P, T], BF16, name=f"plane{j}", tag=f"plane{j}", align_bytes=64)
             if j < 2:
                 nc.vector.tensor_copy(plane[:, 0:HALF], raw[j][:, 0:HALF])
@@ -178,8 +180,9 @@ def tile_moe_res_lin_none_kernel(tc, xT, xr, w_words, w_scales, gate, offs, out)
             nc.vector.tensor_copy(lane(first, j), raw[j][:].indirect(listed(0, SPAN)))
             nc.scalar.activation(lane(mid, j), plane[:].indirect(listed(SPAN, 2 * SPAN)), COPY)
             planes.append(plane)
+
         nc.vector.tensor_copy(lane(first, 3), raw[3][:].indirect(listed(0, SPAN)))
-        deal(0, GROUP, *quantise("first", first, SPAN, "codes0", C))
+        quantise("first", first, 0, GROUP, "codes0", C)
         plane = held.tile([P, T], BF16, name="plane3", tag="first", align_bytes=64)
         nc.vector.tensor_copy(plane[:], raw[3][:])
         planes.append(plane)
@@ -190,57 +193,58 @@ def tile_moe_res_lin_none_kernel(tc, xT, xr, w_words, w_scales, gate, offs, out)
         windows[2] = held.tile([P, T], F32, name="window2", tag="scales_first", align_bytes=64)
         nc.gpsimd.memset(windows[2][:], 0.0)
         scatter_gated(0, back[0], 0)
-        deal(2, 2 * GROUP, *quantise("mid", mid, 2 * SPAN, "back0", 2 * SPAN))
+        quantise("mid", mid, 2, 2 * GROUP, "back0", 2 * SPAN)
         scatter_gated(0, back[1], 1)
         scatter_gated(0, back[2], 2)
-        last = held.tile([P, SPAN * 4], BF16, name="last", tag="codes0", align_bytes=64)
-        for j in range(4):
+        last = held.tile([P, SPAN * PACK], BF16, name="last", tag="codes0", align_bytes=64)
+        for j in range(PACK):
             nc.scalar.activation(lane(last, j), planes[j][:].indirect(listed(3 * SPAN, SPAN)), COPY)
-        deal(6, GROUP, *quantise("last", last, SPAN, "codes3", SPAN))
+        quantise("last", last, 6, GROUP, "codes3", SPAN)
         scatter_gated(0, back[3], 3)
 
-        back = [direct(2, i, f"plane{2 - i}") for i in range(TILES - 1)]
-        gate_turned = psum.tile([P, N], F32, name="turned", bufs=4)
+        back = [direct(2, i, f"plane{2 - i}") for i in range(LAST)]
+        gate_turned = psum.tile([P, N], F32, name="turned", bufs=BANKS)
         nc.tensor.transpose(gate_turned[:, 0:P], gate_rows[:], ident[:])
         gate_cols = held.tile([P, E], F32, name="gate_cols")
-        nc.scalar.copy(gate_cols[:], gate_turned[:, 0:E])
-        for i in range(TILES - 1):
+        nc.scalar.copy(gate_cols[:, 2:E], gate_turned[:, 2:E])
+        for i in range(LAST):
             scatter_gated(2, back[i], i)
+
         for e in range(4, E):
             by_slot([e], 0, N)
-        by_slot([2, 3], (TILES - 1) * P, P)
+        by_slot([2, 3], LAST * P, P)
         for i in range(TILES):
-            s0 = 2 * SPAN if i < TILES - 1 else SPAN
+            s0 = 2 * SPAN if i < LAST else SPAN
             slots = held.tile([P, E * C - s0], F32, name=f"slots{i}")
             turn([4, 5, 6, 7], i, slots[:, 2 * SPAN - s0 :])
-            if i == TILES - 1:
+            if i == LAST:
                 turn([2, 3], i, slots[:, 0:SPAN])
             nc.vector.tensor_copy(windows[i][:].indirect(listed(s0, E * C - s0)), slots[:])
 
-        for i in range(TILES):
+        for i in range(LAST):
             total = held.tile([P, T], F32, name=f"total{i}")
-            if i < TILES - 1:
-                for t0 in range(0, T, HALF):
-                    cols = slice(t0, t0 + HALF)
-                    nc.gpsimd.tensor_tensor(total[:, cols], windows[i][:, cols], residual[i][:, cols], ADD)
-                    nc.sync.dma_start(out[i * P : (i + 1) * P, cols], total[:, cols])
-            else:
-                lines = []
-                for t0, width in PIECES:
-                    upright = psum.tile([P, N], F32, name="turned", bufs=4)
-                    for b in range(0, width, P):
-                        nc.tensor.transpose(upright[:, b : b + P], residual[i][:, t0 + b : t0 + b + P], ident[:])
-                    rows = held.tile([P, width], F32, name=f"rows{t0}")
-                    nc.scalar.copy(rows[:], upright[:, 0:width])
-                    lines.append(rows)
-                for (t0, width), rows in zip(PIECES, lines):
-                    bank = psum.tile([P, N], F32, name="turned", bufs=4)
-                    for b in range(0, width, P):
-                        nc.tensor.transpose(bank[:, b : b + P], rows[:, b : b + P], ident[:])
-                    for c in range(0, width, width // 2):
-                        cols = slice(t0 + c, t0 + c + width // 2)
-                        nc.vector.tensor_tensor(total[:, cols], windows[i][:, cols], bank[:, c : c + width // 2], ADD)
-                        nc.sync.dma_start(out[i * P : (i + 1) * P, cols], total[:, cols])
-                cols = slice(896, T)
+            for t0 in range(0, T, HALF):
+                cols = slice(t0, t0 + HALF)
                 nc.gpsimd.tensor_tensor(total[:, cols], windows[i][:, cols], residual[i][:, cols], ADD)
                 nc.sync.dma_start(out[i * P : (i + 1) * P, cols], total[:, cols])
+
+        total = held.tile([P, T], F32, name=f"total{LAST}")
+        lines = []
+        for t0, width in PIECES:
+            once = psum.tile([P, N], F32, name="turned", bufs=BANKS)
+            for b in range(0, width, P):
+                nc.tensor.transpose(once[:, b : b + P], residual[LAST][:, t0 + b : t0 + b + P], ident[:])
+            line = held.tile([P, width], F32, name=f"rows{t0}")
+            nc.scalar.copy(line[:], once[:, 0:width])
+            lines.append(line)
+        for (t0, width), line in zip(PIECES, lines):
+            twice = psum.tile([P, N], F32, name="turned", bufs=BANKS)
+            for b in range(0, width, P):
+                nc.tensor.transpose(twice[:, b : b + P], line[:, b : b + P], ident[:])
+            for c in range(0, width, width // 2):
+                cols = slice(t0 + c, t0 + c + width // 2)
+                nc.vector.tensor_tensor(total[:, cols], windows[LAST][:, cols], twice[:, c : c + width // 2], ADD)
+                nc.sync.dma_start(out[LAST * P :, cols], total[:, cols])
+        cols = slice(SHARED, T)
+        nc.gpsimd.tensor_tensor(total[:, cols], windows[LAST][:, cols], residual[LAST][:, cols], ADD)
+        nc.sync.dma_start(out[LAST * P :, cols], total[:, cols])

@@ -1,7 +1,6 @@
 from contextlib import ExitStack
 
 import concourse.mybir as mybir
-from concourse.masks import make_identity
 
 K, T, E, C, N = 512, 1280, 8, 128, 512
 FLOPS = 2 * K * N * E * C
@@ -22,20 +21,17 @@ MULT = mybir.AluOpType.mult
 
 PACK = 4
 TILES = N // P
-LAST = TILES - 1
-GROUP = 2
-SPAN = GROUP * C
 HALF = T // 2
-BANKS = 4
-PIECES = [(0, 512), (512, 384)]
-SHARED = 896
+CHUNKS = [(0, 512), (512, 384), (896, 256), (1152, 128)]
+GROUPS = [(0, 2), (2, 3), (5, 3)]
+PIECE = T // 4
 
 
 def tile_moe_res_lin_none_kernel(tc, xT, xr, w_words, w_scales, gate, offs, out):
     nc = tc.nc
     with ExitStack() as ctx:
         held = ctx.enter_context(tc.tile_pool(name="held", bufs=1))
-        psum = ctx.enter_context(tc.psum_pool(name="psum", bufs=BANKS))
+        psum = ctx.enter_context(tc.psum_pool(name="psum", bufs=1))
 
         offsets = held.tile([P, E * C // 16], U16, name="offsets")
         x_rows = xT.rearrange("(p j) t -> p j t", j=PACK)
@@ -43,10 +39,11 @@ def tile_moe_res_lin_none_kernel(tc, xT, xr, w_words, w_scales, gate, offs, out)
         word_rows = w_words.rearrange("e a p b -> (e a) p b")
         scales_w = {}
         words = {}
+        gates = {}
 
-        def load_scales(e0, count, engine):
+        def load_scales(e0, count):
             rows = held.tile([P, count, N], U8, name=f"scales_w{e0}", align_bytes=64)
-            engine.memset(rows[:].rearrange("p e n -> p (e n)").bitcast(I32), 0)
+            nc.vector.memset(rows[:].rearrange("p e n -> p (e n)").bitcast(I32), 0)
             for quad in range(4):
                 nc.sync.dma_start(
                     rows[32 * quad : 32 * quad + 4].bitcast(I32),
@@ -55,196 +52,158 @@ def tile_moe_res_lin_none_kernel(tc, xT, xr, w_words, w_scales, gate, offs, out)
             for k in range(count):
                 scales_w[e0 + k] = rows[:, k, :]
 
-        def load_words(e0):
-            pair = held.tile([P, GROUP, 2 * N], U8, name=f"words{e0}", align_bytes=64)
+        def load_words(g):
+            e0, count = GROUPS[g]
+            group = held.tile([P, count, 2 * N], U8, name=f"words{g}", align_bytes=64)
             nc.sync.dma_start(
-                pair[:].bitcast(I32), word_rows[e0 : e0 + GROUP].bitcast(I32).rearrange("e p b -> p e b")
+                group[:].bitcast(I32), word_rows[e0 : e0 + count].bitcast(I32).rearrange("e p b -> p e b")
             )
-            for k in range(GROUP):
-                words[e0 + k] = pair[:, k, :]
+            for k in range(count):
+                words[e0 + k] = group[:, k, :]
 
-        raw = [held.tile([P, T], F32, name=f"raw{j}", tag=f"raw{j}", align_bytes=64) for j in range(PACK)]
-        for j in range(2):
-            nc.sync.dma_start(raw[j][:, 0:HALF], x_rows[:, j, 0:HALF])
-            nc.sync.dma_start(raw[j][:, HALF:T], x_rows[:, j, HALF:T])
-            if j == 0:
+        def load_gate(g):
+            e0, count = GROUPS[g]
+            gates[g] = held.tile([P, count * C], F32, name=f"gate{g}")
+            nc.sync.dma_start(gates[g][:], gate[0:P, e0 * C : (e0 + count) * C])
+
+        raw = []
+        for c, (t0, width) in enumerate(CHUNKS):
+            chunk = held.tile([P, PACK, width], F32, name=f"raw{c}")
+            nc.sync.dma_start(chunk[:], x_rows[:, :, t0 : t0 + width])
+            raw.append(chunk)
+            if c == 0:
                 nc.sync.dma_start(offsets[:], offs)
-        nc.sync.dma_start(raw[2][:], x_rows[:, 2, :])
-        load_scales(0, GROUP, nc.vector)
-        nc.sync.dma_start(raw[3][:], x_rows[:, 3, :])
+        load_scales(0, 2)
         load_words(0)
-        gate_wide = held.tile([P, 2 * SPAN], F32, name="gate_wide")
-        nc.sync.dma_start(gate_wide[:], gate[0:P, 0 : 2 * SPAN])
+        load_gate(0)
+        load_words(1)
+        load_scales(2, E - 2)
+        load_gate(1)
         load_words(2)
-        load_scales(GROUP, E - GROUP, nc.gpsimd)
-        gate_rows = held.tile([P, P], F32, name="gate_rows")
-        nc.gpsimd.memset(gate_rows[:], 0.0)
-        by_expert = gate[0:1, :].rearrange("r (e c) -> (r e) c", e=E)
-        nc.sync.dma_start(gate_rows[4:E, :], by_expert[4:E])
-        nc.sync.dma_start(gate_rows[2:4, :], by_expert[2:4])
-        load_words(4)
-        load_words(6)
-        residual = []
+        load_gate(2)
+        residual = {}
         for i in range(TILES):
-            xr_tile = held.tile([P, T], F32, name=f"xr{i}")
-            nc.sync.dma_start(xr_tile[:], xr[i * P : (i + 1) * P, :])
-            residual.append(xr_tile)
+            for h in range(2):
+                residual[i, h] = held.tile([P, HALF], F32, name=f"xr{i}_{h}", tag=f"xr{i}_{h}")
+                nc.sync.dma_start(residual[i, h][:], xr[i * P : (i + 1) * P, h * HALF : (h + 1) * HALF])
 
-        ident = held.tile([P, P], F32, name="ident")
-        make_identity(nc, ident[:])
-        windows = {i: held.tile([P, T], F32, name=f"window{i}") for i in (0, 1, LAST)}
+        codes = held.tile([P, T], U32, name="codes", align_bytes=64)
+        scales = held.tile([P, T], U8, name="scales", align_bytes=64)
+        windows = [held.tile([P, T], F32, name=f"window{i}") for i in range(TILES)]
         nc.vector.memset(windows[0][:], 0.0)
+        nc.vector.memset(scales[:].bitcast(I32), 0)
         nc.vector.memset(windows[1][:], 0.0)
-        nc.scalar.copy(windows[LAST][:], windows[0][:])
+        nc.gpsimd.memset(windows[2][:], 0.0)
+        nc.scalar.copy(windows[3][:], windows[0][:])
+
+        for c, (t0, width) in enumerate(CHUNKS):
+            rounded = held.tile([P, width, PACK], BF16, name=f"rounded{c}", align_bytes=64)
+            by_token = raw[c][:].rearrange("p j t -> p t j")
+            mid = width // 2
+            nc.scalar.activation(rounded[:, mid:width, :], by_token[:, mid:width, :], COPY)
+            nc.vector.tensor_copy(rounded[:, 0:mid, :], by_token[:, 0:mid, :])
+            nc.vector.quantize_mx(
+                out=codes[:, t0 : t0 + width].bitcast(E4M3),
+                scales=scales[:, t0 : t0 + width],
+                in_=rounded[:].rearrange("p t j -> p (t j)"),
+            )
 
         def listed(s0, count):
             return offsets[:, s0 // 16 : (s0 + count) // 16]
 
-        def lane(target, j):
-            return target[:].rearrange("p (s j) -> p s j", j=PACK)[:, :, j]
+        slot_codes = {}
+        slot_scales = {}
 
-        tokens = {}
+        def gather_codes(g, tag):
+            e0, count = GROUPS[g]
+            slot_codes[g] = held.tile([P, count * C], U32, name=f"slot_codes{g}", tag=tag, align_bytes=64)
+            nc.vector.tensor_copy(slot_codes[g][:], codes[:].indirect(listed(e0 * C, count * C)))
 
-        def quantise(name, source, e0, count, tag, step):
-            width = count * C
-            codes = held.tile([P, width], U32, name=f"codes_{name}", tag=tag, align_bytes=64)
-            scales = held.tile([P, width], U8, name=f"scales_{name}", tag=f"scales_{name}", align_bytes=64)
-            for s0 in range(0, width, step):
-                nc.vector.quantize_mx(
-                    out=codes[:, s0 : s0 + step].bitcast(E4M3),
-                    scales=scales[:, s0 : s0 + step],
-                    in_=source[:, PACK * s0 : PACK * (s0 + step)],
-                )
+        def gather_scales(g):
+            e0, count = GROUPS[g]
+            slot_scales[g] = held.tile([P, count * C], U8, name=f"slot_scales{g}", tag="slot_scales", align_bytes=64)
+            nc.vector.tensor_copy(slot_scales[g][:], scales[:].indirect(listed(e0 * C, count * C)))
+
+        sums = {}
+
+        def multiply(g, i, bank):
+            e0, count = GROUPS[g]
+            sums[g, i] = psum.tile([P, N], F32, name=f"sums{g}_{i}", tag=f"bank{bank}")
             for k in range(count):
-                tokens[e0 + k] = (codes[:, k * C : (k + 1) * C].bitcast(E4M3), scales[:, k * C : (k + 1) * C])
-
-        def direct(e0, i, tag, step=GROUP):
-            slots = held.tile([P, SPAN], F32, name=f"direct{e0}_{i}", tag=tag, align_bytes=64)
-            for k0 in range(0, GROUP, step):
-                acc = psum.tile([P, N], F32, name="acc", bufs=BANKS)
-                for k in range(step):
-                    e = e0 + k0 + k
-                    nc.tensor.matmul_mx(
-                        out=acc[:, k * C : (k + 1) * C],
-                        lhsT=words[e][:, 2 * i * P : 2 * (i + 1) * P].bitcast(E2M1),
-                        lhsT_scale=scales_w[e][:, i * P : (i + 1) * P],
-                        rhs=tokens[e][0],
-                        rhs_scale=tokens[e][1],
-                        start=True,
-                        stop=True,
-                    )
-                nc.scalar.copy(slots[:, k0 * C : (k0 + step) * C], acc[:, 0 : step * C])
-            return slots
-
-        def scatter_gated(e0, slots, i):
-            nc.vector.tensor_tensor(
-                windows[i][:].indirect(listed(e0 * C, SPAN)), slots[:], gate_wide[:, e0 * C : e0 * C + SPAN], MULT
-            )
-
-        gated = {}
-
-        def by_slot(experts, n0, width):
-            acc = psum.tile([P, N], F32, name="acc", bufs=BANKS)
-            for k, e in enumerate(experts):
+                e = e0 + k
                 nc.tensor.matmul_mx(
-                    out=acc[:, k * width : (k + 1) * width],
-                    lhsT=tokens[e][0],
-                    lhsT_scale=tokens[e][1],
-                    rhs=words[e][:, 2 * n0 : 2 * (n0 + width)].bitcast(E2M1),
-                    rhs_scale=scales_w[e][:, n0 : n0 + width],
+                    out=sums[g, i][:, k * C : (k + 1) * C],
+                    lhsT=words[e][:, 2 * i * P : 2 * (i + 1) * P].bitcast(E2M1),
+                    lhsT_scale=scales_w[e][:, i * P : (i + 1) * P],
+                    rhs=slot_codes[g][:, k * C : (k + 1) * C].bitcast(E4M3),
+                    rhs_scale=slot_scales[g][:, k * C : (k + 1) * C],
                     start=True,
                     stop=True,
                 )
-            for k, e in enumerate(experts):
-                rows = held.tile([P, width], F32, name=f"gated{e}")
-                nc.scalar.activation(rows[:], acc[:, k * width : (k + 1) * width], COPY, scale=gate_cols[:, e : e + 1])
-                gated[e] = (rows, n0)
 
-        def turn(experts, i, target):
-            turned = psum.tile([P, N], F32, name="turned", bufs=BANKS)
-            for k, e in enumerate(experts):
-                rows, n0 = gated[e]
-                nc.tensor.transpose(turned[:, k * C : (k + 1) * C], rows[:, i * P - n0 : (i + 1) * P - n0], ident[:])
-            nc.scalar.copy(target, turned[:, 0 : len(experts) * C])
+        gated = {}
 
-        first = held.tile([P, SPAN * PACK], BF16, name="first", tag="first", align_bytes=64)
-        mid = held.tile([P, 2 * SPAN * PACK], BF16, name="mid", align_bytes=64)
-        planes = []
-        for j in range(PACK - 1):
-            plane = held.tile([P, T], BF16, name=f"plane{j}", tag=f"plane{j}", align_bytes=64)
-            if j < 2:
-                nc.vector.tensor_copy(plane[:, 0:HALF], raw[j][:, 0:HALF])
-                nc.vector.tensor_copy(plane[:, HALF:T], raw[j][:, HALF:T])
-            else:
-                nc.vector.tensor_copy(plane[:], raw[j][:])
-            nc.vector.tensor_copy(lane(first, j), raw[j][:].indirect(listed(0, SPAN)))
-            nc.scalar.activation(lane(mid, j), plane[:].indirect(listed(SPAN, 2 * SPAN)), COPY)
-            planes.append(plane)
+        def weigh(g, i, tag=None):
+            count = GROUPS[g][1]
+            gated[g, i] = held.tile([P, count * C], F32, name=f"gated{g}_{i}", tag=tag or f"gated{g}_{i}")
+            nc.vector.tensor_tensor(gated[g, i][:], sums[g, i][:, 0 : count * C], gates[g][:], MULT)
 
-        nc.vector.tensor_copy(lane(first, 3), raw[3][:].indirect(listed(0, SPAN)))
-        quantise("first", first, 0, GROUP, "codes0", C)
-        plane = held.tile([P, T], BF16, name="plane3", tag="first", align_bytes=64)
-        nc.vector.tensor_copy(plane[:], raw[3][:])
-        planes.append(plane)
+        def scatter_scalar(g, i):
+            e0, count = GROUPS[g]
+            nc.scalar.activation(windows[i][:].indirect(listed(e0 * C, count * C)), gated[g, i][:], COPY)
 
-        back = [direct(0, 0, "back0", 1), direct(0, 1, "back1")]
-        nc.scalar.activation(lane(mid, 3), planes[3][:].indirect(listed(SPAN, 2 * SPAN)), COPY)
-        back.extend([direct(0, 2, "raw3"), direct(0, 3, "back3")])
-        windows[2] = held.tile([P, T], F32, name="window2", tag="scales_first", align_bytes=64)
-        nc.gpsimd.memset(windows[2][:], 0.0)
-        scatter_gated(0, back[0], 0)
-        quantise("mid", mid, 2, 2 * GROUP, "back0", 2 * SPAN)
-        scatter_gated(0, back[1], 1)
-        scatter_gated(0, back[2], 2)
-        last = held.tile([P, SPAN * PACK], BF16, name="last", tag="codes0", align_bytes=64)
-        for j in range(PACK):
-            nc.scalar.activation(lane(last, j), planes[j][:].indirect(listed(3 * SPAN, SPAN)), COPY)
-        quantise("last", last, 6, GROUP, "codes3", SPAN)
-        scatter_gated(0, back[3], 3)
+        def scatter_vector(g, i):
+            e0, count = GROUPS[g]
+            nc.vector.tensor_copy(windows[i][:].indirect(listed(e0 * C, count * C)), gated[g, i][:])
 
-        back = [direct(2, i, f"plane{2 - i}") for i in range(LAST)]
-        gate_turned = psum.tile([P, N], F32, name="turned", bufs=BANKS)
-        nc.tensor.transpose(gate_turned[:, 0:P], gate_rows[:], ident[:])
-        gate_cols = held.tile([P, E], F32, name="gate_cols")
-        nc.scalar.copy(gate_cols[:, 2:E], gate_turned[:, 2:E])
-        for i in range(LAST):
-            scatter_gated(2, back[i], i)
-
-        for e in range(4, E):
-            by_slot([e], 0, N)
-        by_slot([2, 3], LAST * P, P)
+        gather_scales(0)
+        gather_codes(0, "codes_a")
+        gather_codes(1, "codes_b")
         for i in range(TILES):
-            s0 = 2 * SPAN if i < LAST else SPAN
-            slots = held.tile([P, E * C - s0], F32, name=f"slots{i}")
-            turn([4, 5, 6, 7], i, slots[:, 2 * SPAN - s0 :])
-            if i == LAST:
-                turn([2, 3], i, slots[:, 0:SPAN])
-            nc.vector.tensor_copy(windows[i][:].indirect(listed(s0, E * C - s0)), slots[:])
+            multiply(0, i, i)
+        weigh(0, 0)
+        scatter_scalar(0, 0)
+        weigh(0, 1)
+        scatter_scalar(0, 1)
+        gather_scales(1)
+        gather_codes(2, "codes_a")
+        for i in range(TILES):
+            multiply(1, i, TILES + i)
+        weigh(1, 0)
+        scatter_scalar(1, 0)
+        weigh(1, 1)
+        gather_scales(2)
+        weigh(0, 2)
+        for i, bank in enumerate([0, 1, 4, 5]):
+            multiply(2, i, bank)
+        weigh(2, 0)
+        scatter_scalar(2, 0)
+        weigh(2, 1)
+        scatter_vector(2, 1)
+        scatter_scalar(1, 1)
+        weigh(1, 2)
+        weigh(2, 2)
+        for g in range(3):
+            weigh(g, 3, "gated2_1" if g == 0 else None)
+            scatter_scalar(g, 3)
+        for g in (2, 1, 0):
+            scatter_vector(g, 2)
 
-        for i in range(LAST):
+        for i in range(2):
             total = held.tile([P, T], F32, name=f"total{i}")
-            for t0 in range(0, T, HALF):
-                cols = slice(t0, t0 + HALF)
-                nc.gpsimd.tensor_tensor(total[:, cols], windows[i][:, cols], residual[i][:, cols], ADD)
+            for h in range(2):
+                cols = slice(h * HALF, (h + 1) * HALF)
+                nc.gpsimd.tensor_tensor(total[:, cols], windows[i][:, cols], residual[i, h][:], ADD)
                 nc.sync.dma_start(out[i * P : (i + 1) * P, cols], total[:, cols])
-
-        total = held.tile([P, T], F32, name=f"total{LAST}")
-        lines = []
-        for t0, width in PIECES:
-            once = psum.tile([P, N], F32, name="turned", bufs=BANKS)
-            for b in range(0, width, P):
-                nc.tensor.transpose(once[:, b : b + P], residual[LAST][:, t0 + b : t0 + b + P], ident[:])
-            line = held.tile([P, width], F32, name=f"rows{t0}")
-            nc.scalar.copy(line[:], once[:, 0:width])
-            lines.append(line)
-        for (t0, width), line in zip(PIECES, lines):
-            twice = psum.tile([P, N], F32, name="turned", bufs=BANKS)
-            for b in range(0, width, P):
-                nc.tensor.transpose(twice[:, b : b + P], line[:, b : b + P], ident[:])
-            for c in range(0, width, width // 2):
-                cols = slice(t0 + c, t0 + c + width // 2)
-                nc.vector.tensor_tensor(total[:, cols], windows[LAST][:, cols], twice[:, c : c + width // 2], ADD)
-                nc.sync.dma_start(out[LAST * P :, cols], total[:, cols])
-        cols = slice(SHARED, T)
-        nc.gpsimd.tensor_tensor(total[:, cols], windows[LAST][:, cols], residual[LAST][:, cols], ADD)
-        nc.sync.dma_start(out[LAST * P :, cols], total[:, cols])
+        total = held.tile([P, T], F32, name="total2", tag="xr1_1")
+        for h in range(2):
+            cols = slice(h * HALF, (h + 1) * HALF)
+            nc.vector.tensor_tensor(total[:, cols], windows[2][:, cols], residual[2, h][:], ADD)
+            nc.sync.dma_start(out[2 * P : 3 * P, cols], total[:, cols])
+        total = held.tile([P, T], F32, name="total3", tag="xr2_0")
+        for t0 in range(0, T, PIECE):
+            cols = slice(t0, t0 + PIECE)
+            h = t0 // HALF
+            part = residual[3, h][:, t0 - h * HALF : t0 - h * HALF + PIECE]
+            nc.vector.tensor_tensor(total[:, cols], windows[3][:, cols], part, ADD)
+            nc.sync.dma_start(out[3 * P :, cols], total[:, cols])

@@ -22,9 +22,12 @@ MULT = mybir.AluOpType.mult
 PACK = 4
 TILES = N // P
 HALF = T // 2
-CHUNKS = [(0, 512), (512, 384), (896, 256), (1152, 128)]
 GROUPS = [(0, 2), (2, 3), (5, 3)]
 PIECE = T // 4
+EARLY = 192
+WOVEN = 256
+FILL = 160
+SHARE = 544
 
 
 def tile_moe_res_lin_none_kernel(tc, xT, xr, w_words, w_scales, gate, offs, out):
@@ -41,9 +44,9 @@ def tile_moe_res_lin_none_kernel(tc, xT, xr, w_words, w_scales, gate, offs, out)
         words = {}
         gates = {}
 
-        def load_scales(e0, count):
+        def load_scales(e0, count, engine):
             rows = held.tile([P, count, N], U8, name=f"scales_w{e0}", align_bytes=64)
-            nc.vector.memset(rows[:].rearrange("p e n -> p (e n)").bitcast(I32), 0)
+            engine.memset(rows[:].rearrange("p e n -> p (e n)").bitcast(I32), 0)
             for quad in range(4):
                 nc.sync.dma_start(
                     rows[32 * quad : 32 * quad + 4].bitcast(I32),
@@ -66,63 +69,57 @@ def tile_moe_res_lin_none_kernel(tc, xT, xr, w_words, w_scales, gate, offs, out)
             gates[g] = held.tile([P, count * C], F32, name=f"gate{g}")
             nc.sync.dma_start(gates[g][:], gate[0:P, e0 * C : (e0 + count) * C])
 
-        raw = []
-        for c, (t0, width) in enumerate(CHUNKS):
-            chunk = held.tile([P, PACK, width], F32, name=f"raw{c}")
-            nc.sync.dma_start(chunk[:], x_rows[:, :, t0 : t0 + width])
-            raw.append(chunk)
-            if c == 0:
+        planes = []
+        for j in range(PACK):
+            plane = held.tile([P, T], F32, name=f"plane{j}")
+            nc.sync.dma_start(plane[:], x_rows[:, j, :])
+            planes.append(plane)
+            if j == 0:
                 nc.sync.dma_start(offsets[:], offs)
-        load_scales(0, 2)
+        load_scales(0, 2, nc.vector)
         load_words(0)
         load_gate(0)
         load_words(1)
-        load_scales(2, E - 2)
+        load_scales(2, E - 2, nc.gpsimd)
         load_gate(1)
         load_words(2)
         load_gate(2)
         residual = {}
-        for i in range(TILES):
+        for i in (1, 0, 2, 3):
             for h in range(2):
                 residual[i, h] = held.tile([P, HALF], F32, name=f"xr{i}_{h}", tag=f"xr{i}_{h}")
                 nc.sync.dma_start(residual[i, h][:], xr[i * P : (i + 1) * P, h * HALF : (h + 1) * HALF])
 
-        codes = held.tile([P, T], U32, name="codes", align_bytes=64)
-        scales = held.tile([P, T], U8, name="scales", align_bytes=64)
-        windows = [held.tile([P, T], F32, name=f"window{i}") for i in range(TILES)]
+        windows = {i: held.tile([P, T], F32, name=f"window{i}") for i in range(3)}
         nc.vector.memset(windows[0][:], 0.0)
-        nc.vector.memset(scales[:].bitcast(I32), 0)
         nc.vector.memset(windows[1][:], 0.0)
-        nc.gpsimd.memset(windows[2][:], 0.0)
-        nc.scalar.copy(windows[3][:], windows[0][:])
-
-        for c, (t0, width) in enumerate(CHUNKS):
-            rounded = held.tile([P, width, PACK], BF16, name=f"rounded{c}", align_bytes=64)
-            by_token = raw[c][:].rearrange("p j t -> p t j")
-            mid = width // 2
-            nc.scalar.activation(rounded[:, mid:width, :], by_token[:, mid:width, :], COPY)
-            nc.vector.tensor_copy(rounded[:, 0:mid, :], by_token[:, 0:mid, :])
-            nc.vector.quantize_mx(
-                out=codes[:, t0 : t0 + width].bitcast(E4M3),
-                scales=scales[:, t0 : t0 + width],
-                in_=rounded[:].rearrange("p t j -> p (t j)"),
-            )
+        nc.scalar.copy(windows[2][:], windows[0][:])
 
         def listed(s0, count):
             return offsets[:, s0 // 16 : (s0 + count) // 16]
 
-        slot_codes = {}
-        slot_scales = {}
+        woven = {0: held.tile([P, 2 * C, PACK], BF16, name="woven0", tag="woven", align_bytes=64)}
+        flat = {g: held.tile([P, PACK, 3 * C], BF16, name=f"flat{g}", align_bytes=64) for g in (1, 2)}
+        for j in range(PACK):
+            early = EARLY if j < PACK - 1 else 0
+            nc.vector.tensor_copy(woven[0][:, :, j], planes[j][:].indirect(listed(0, 2 * C)))
+            if early:
+                nc.vector.tensor_copy(flat[1][:, j, 0:early], planes[j][:].indirect(listed(2 * C, early)))
+            nc.scalar.activation(
+                flat[1][:, j, early : 3 * C], planes[j][:].indirect(listed(2 * C + early, 3 * C - early)), COPY
+            )
+            nc.scalar.activation(flat[2][:, j, :], planes[j][:].indirect(listed(5 * C, 3 * C)), COPY)
 
-        def gather_codes(g, tag):
-            e0, count = GROUPS[g]
-            slot_codes[g] = held.tile([P, count * C], U32, name=f"slot_codes{g}", tag=tag, align_bytes=64)
-            nc.vector.tensor_copy(slot_codes[g][:], codes[:].indirect(listed(e0 * C, count * C)))
+        codes = {}
+        scales = {}
 
-        def gather_scales(g):
-            e0, count = GROUPS[g]
-            slot_scales[g] = held.tile([P, count * C], U8, name=f"slot_scales{g}", tag="slot_scales", align_bytes=64)
-            nc.vector.tensor_copy(slot_scales[g][:], scales[:].indirect(listed(e0 * C, count * C)))
+        def quantise(g):
+            width = GROUPS[g][1] * C
+            codes[g] = held.tile([P, width], U32, name=f"codes{g}", tag="codes", align_bytes=64)
+            scales[g] = held.tile([P, width], U8, name=f"scales{g}", align_bytes=64)
+            nc.vector.quantize_mx(
+                out=codes[g][:].bitcast(E4M3), scales=scales[g][:], in_=woven[g][:].rearrange("p s j -> p (s j)")
+            )
 
         sums = {}
 
@@ -135,75 +132,81 @@ def tile_moe_res_lin_none_kernel(tc, xT, xr, w_words, w_scales, gate, offs, out)
                     out=sums[g, i][:, k * C : (k + 1) * C],
                     lhsT=words[e][:, 2 * i * P : 2 * (i + 1) * P].bitcast(E2M1),
                     lhsT_scale=scales_w[e][:, i * P : (i + 1) * P],
-                    rhs=slot_codes[g][:, k * C : (k + 1) * C].bitcast(E4M3),
-                    rhs_scale=slot_scales[g][:, k * C : (k + 1) * C],
+                    rhs=codes[g][:, k * C : (k + 1) * C].bitcast(E4M3),
+                    rhs_scale=scales[g][:, k * C : (k + 1) * C],
                     start=True,
                     stop=True,
                 )
 
-        gated = {}
+        gated = [held.tile([P, E * C], F32, name=f"gated{i}") for i in range(TILES - 1)]
+        last = {}
 
         def weigh(g, i, tag=None):
-            count = GROUPS[g][1]
-            gated[g, i] = held.tile([P, count * C], F32, name=f"gated{g}_{i}", tag=tag or f"gated{g}_{i}")
-            nc.vector.tensor_tensor(gated[g, i][:], sums[g, i][:, 0 : count * C], gates[g][:], MULT)
-
-        def scatter_scalar(g, i):
             e0, count = GROUPS[g]
-            nc.scalar.activation(windows[i][:].indirect(listed(e0 * C, count * C)), gated[g, i][:], COPY)
+            if i == TILES - 1:
+                last[g] = held.tile([P, count * C], F32, name=f"last{g}", tag=tag or f"last{g}", align_bytes=64)
+                target = last[g][:]
+            else:
+                target = gated[i][:, e0 * C : (e0 + count) * C]
+            nc.vector.tensor_tensor(target, sums[g, i][:, 0 : count * C], gates[g][:], MULT)
 
-        def scatter_vector(g, i):
-            e0, count = GROUPS[g]
-            nc.vector.tensor_copy(windows[i][:].indirect(listed(e0 * C, count * C)), gated[g, i][:])
+        def scatter_scalar(i, s0, s1):
+            nc.scalar.activation(windows[i][:].indirect(listed(s0, s1 - s0)), gated[i][:, s0:s1], COPY)
 
-        gather_scales(0)
-        gather_codes(0, "codes_a")
-        gather_codes(1, "codes_b")
-        for i in range(TILES):
+        def scatter_vector(i, s0, s1):
+            nc.vector.tensor_copy(windows[i][:].indirect(listed(s0, s1 - s0)), gated[i][:, s0:s1])
+
+        quantise(0)
+        woven[1] = held.tile([P, 3 * C, PACK], BF16, name="woven1", tag="woven", align_bytes=64)
+        by_slot = flat[1][:].rearrange("p j s -> p s j")
+        nc.vector.tensor_copy(woven[1][:, 0:WOVEN, :], by_slot[:, 0:WOVEN, :])
+        nc.scalar.copy(woven[1][:, WOVEN:, :], by_slot[:, WOVEN:, :])
+        for i in (0, 1, 3, 2):
             multiply(0, i, i)
         weigh(0, 0)
-        scatter_scalar(0, 0)
+        scatter_scalar(0, 0, 2 * C)
         weigh(0, 1)
-        scatter_scalar(0, 1)
-        gather_scales(1)
-        gather_codes(2, "codes_a")
-        for i in range(TILES):
-            multiply(1, i, TILES + i)
-        weigh(1, 0)
-        scatter_scalar(1, 0)
-        weigh(1, 1)
-        gather_scales(2)
+        scatter_scalar(1, 0, 2 * C)
+        weigh(0, 3)
+        quantise(1)
+        woven[2] = held.tile([P, 3 * C, PACK], BF16, name="woven2", tag="woven", align_bytes=64)
+        nc.gpsimd.tensor_scalar(woven[2][:], flat[2][:].rearrange("p j s -> p s j"), 1.0, 0.0, MULT, ADD)
         weigh(0, 2)
-        for i, bank in enumerate([0, 1, 4, 5]):
-            multiply(2, i, bank)
-        weigh(2, 0)
-        scatter_scalar(2, 0)
-        weigh(2, 1)
-        scatter_vector(2, 1)
-        scatter_scalar(1, 1)
+        scatter_vector(2, 0, FILL)
+        for i in (1, 0, 3, 2):
+            multiply(1, i, TILES + i)
+        weigh(1, 1)
+        scatter_scalar(1, 2 * C, E * C - SHARE)
+        weigh(1, 0)
+        scatter_scalar(0, 2 * C, 5 * C)
+        quantise(2)
+        weigh(1, 3, "woven")
         weigh(1, 2)
+        for i in range(TILES):
+            multiply(2, i, i)
+        windows[3] = held.tile([P, T], F32, name="window3", tag="codes", align_bytes=64)
+        nc.gpsimd.memset(windows[3][:], 0.0)
+        weigh(2, 0)
+        scatter_scalar(0, 5 * C, E * C)
+        weigh(2, 1)
+        scatter_vector(1, E * C - SHARE, E * C)
         weigh(2, 2)
-        for g in range(3):
-            weigh(g, 3, "gated2_1" if g == 0 else None)
-            scatter_scalar(g, 3)
-        for g in (2, 1, 0):
-            scatter_vector(g, 2)
+        weigh(2, 3)
+        for g, (e0, count) in enumerate(GROUPS):
+            nc.scalar.activation(windows[3][:].indirect(listed(e0 * C, count * C)), last[g][:], COPY)
+        scatter_vector(2, FILL, E * C)
 
-        for i in range(2):
+        for i in (1, 0):
             total = held.tile([P, T], F32, name=f"total{i}")
             for h in range(2):
                 cols = slice(h * HALF, (h + 1) * HALF)
                 nc.gpsimd.tensor_tensor(total[:, cols], windows[i][:, cols], residual[i, h][:], ADD)
                 nc.sync.dma_start(out[i * P : (i + 1) * P, cols], total[:, cols])
-        total = held.tile([P, T], F32, name="total2", tag="xr1_1")
-        for h in range(2):
-            cols = slice(h * HALF, (h + 1) * HALF)
-            nc.vector.tensor_tensor(total[:, cols], windows[2][:, cols], residual[2, h][:], ADD)
-            nc.sync.dma_start(out[2 * P : 3 * P, cols], total[:, cols])
-        total = held.tile([P, T], F32, name="total3", tag="xr2_0")
-        for t0 in range(0, T, PIECE):
-            cols = slice(t0, t0 + PIECE)
-            h = t0 // HALF
-            part = residual[3, h][:, t0 - h * HALF : t0 - h * HALF + PIECE]
-            nc.vector.tensor_tensor(total[:, cols], windows[3][:, cols], part, ADD)
-            nc.sync.dma_start(out[3 * P :, cols], total[:, cols])
+        for i, tag in ((2, "xr0_1"), (3, "xr2_0")):
+            total = held.tile([P, T], F32, name=f"total{i}", tag=tag)
+            for t0 in range(0, T, PIECE):
+                cols = slice(t0, t0 + PIECE)
+                h = t0 // HALF
+                part = residual[i, h][:, t0 - h * HALF : t0 - h * HALF + PIECE]
+                nc.vector.tensor_tensor(total[:, cols], windows[i][:, cols], part, ADD)
+                nc.sync.dma_start(out[i * P : (i + 1) * P, cols], total[:, cols])

from contextlib import ExitStack

import concourse.mybir as mybir

K, T, E, C, N = 512, 1280, 8, 128, 512
FLOPS = 2 * K * N * E * C
BYTES = 4 * (K * T + 2 * N * T + E * C) + E * K * N // 2 + E * 16 * N + 2 * E * C

P = 128
F32 = mybir.dt.float32
BF16 = mybir.dt.bfloat16
I32 = mybir.dt.int32
U32 = mybir.dt.uint32
U16 = mybir.dt.uint16
U8 = mybir.dt.uint8
E4M3 = mybir.dt.float8_e4m3fn_x4
E2M1 = mybir.dt.float4_e2m1fn_x4
COPY = mybir.ActivationFunctionType.Copy
ADD = mybir.AluOpType.add
MULT = mybir.AluOpType.mult

PACK = 4
TILES = N // P
HALF = T // 2
GROUPS = [(0, 2), (2, 3), (5, 3)]
PIECE = T // 4
EARLY = 192
WOVEN = 256
FILL = 160
SHARE = 544


def tile_moe_res_lin_none_kernel(tc, xT, xr, w_words, w_scales, gate, offs, out):
    nc = tc.nc
    with ExitStack() as ctx:
        held = ctx.enter_context(tc.tile_pool(name="held", bufs=1))
        psum = ctx.enter_context(tc.psum_pool(name="psum", bufs=1))

        offsets = held.tile([P, E * C // 16], U16, name="offsets")
        x_rows = xT.rearrange("(p j) t -> p j t", j=PACK)
        scale_rows = w_scales.rearrange("e a q n -> (e a) q n")
        word_rows = w_words.rearrange("e a p b -> (e a) p b")
        scales_w = {}
        words = {}
        gates = {}

        def load_scales(e0, count, engine):
            rows = held.tile([P, count, N], U8, name=f"scales_w{e0}", align_bytes=64)
            engine.memset(rows[:].rearrange("p e n -> p (e n)").bitcast(I32), 0)
            for quad in range(4):
                nc.sync.dma_start(
                    rows[32 * quad : 32 * quad + 4].bitcast(I32),
                    scale_rows[e0 : e0 + count, 4 * quad : 4 * quad + 4, :].bitcast(I32).rearrange("e q n -> q e n"),
                )
            for k in range(count):
                scales_w[e0 + k] = rows[:, k, :]

        def load_words(g):
            e0, count = GROUPS[g]
            group = held.tile([P, count, 2 * N], U8, name=f"words{g}", align_bytes=64)
            nc.sync.dma_start(
                group[:].bitcast(I32), word_rows[e0 : e0 + count].bitcast(I32).rearrange("e p b -> p e b")
            )
            for k in range(count):
                words[e0 + k] = group[:, k, :]

        def load_gate(g):
            e0, count = GROUPS[g]
            gates[g] = held.tile([P, count * C], F32, name=f"gate{g}")
            nc.sync.dma_start(gates[g][:], gate[0:P, e0 * C : (e0 + count) * C])

        planes = []
        for j in range(PACK):
            plane = held.tile([P, T], F32, name=f"plane{j}")
            nc.sync.dma_start(plane[:], x_rows[:, j, :])
            planes.append(plane)
            if j == 0:
                nc.sync.dma_start(offsets[:], offs)
        load_scales(0, 2, nc.vector)
        load_words(0)
        load_gate(0)
        load_words(1)
        load_scales(2, E - 2, nc.gpsimd)
        load_gate(1)
        load_words(2)
        load_gate(2)
        residual = {}
        for i in (1, 0, 2, 3):
            for h in range(2):
                residual[i, h] = held.tile([P, HALF], F32, name=f"xr{i}_{h}", tag=f"xr{i}_{h}")
                nc.sync.dma_start(residual[i, h][:], xr[i * P : (i + 1) * P, h * HALF : (h + 1) * HALF])

        windows = {i: held.tile([P, T], F32, name=f"window{i}") for i in range(3)}
        nc.vector.memset(windows[0][:], 0.0)
        nc.vector.memset(windows[1][:], 0.0)
        nc.scalar.copy(windows[2][:], windows[0][:])

        def listed(s0, count):
            return offsets[:, s0 // 16 : (s0 + count) // 16]

        woven = {0: held.tile([P, 2 * C, PACK], BF16, name="woven0", tag="woven", align_bytes=64)}
        flat = {g: held.tile([P, PACK, 3 * C], BF16, name=f"flat{g}", align_bytes=64) for g in (1, 2)}
        for j in range(PACK):
            early = EARLY if j < PACK - 1 else 0
            nc.vector.tensor_copy(woven[0][:, :, j], planes[j][:].indirect(listed(0, 2 * C)))
            if early:
                nc.vector.tensor_copy(flat[1][:, j, 0:early], planes[j][:].indirect(listed(2 * C, early)))
            nc.scalar.activation(
                flat[1][:, j, early : 3 * C], planes[j][:].indirect(listed(2 * C + early, 3 * C - early)), COPY
            )
            nc.scalar.activation(flat[2][:, j, :], planes[j][:].indirect(listed(5 * C, 3 * C)), COPY)

        codes = {}
        scales = {}

        def quantise(g):
            width = GROUPS[g][1] * C
            codes[g] = held.tile([P, width], U32, name=f"codes{g}", tag="codes", align_bytes=64)
            scales[g] = held.tile([P, width], U8, name=f"scales{g}", align_bytes=64)
            nc.vector.quantize_mx(
                out=codes[g][:].bitcast(E4M3), scales=scales[g][:], in_=woven[g][:].rearrange("p s j -> p (s j)")
            )

        sums = {}

        def multiply(g, i, bank):
            e0, count = GROUPS[g]
            sums[g, i] = psum.tile([P, N], F32, name=f"sums{g}_{i}", tag=f"bank{bank}")
            for k in range(count):
                e = e0 + k
                nc.tensor.matmul_mx(
                    out=sums[g, i][:, k * C : (k + 1) * C],
                    lhsT=words[e][:, 2 * i * P : 2 * (i + 1) * P].bitcast(E2M1),
                    lhsT_scale=scales_w[e][:, i * P : (i + 1) * P],
                    rhs=codes[g][:, k * C : (k + 1) * C].bitcast(E4M3),
                    rhs_scale=scales[g][:, k * C : (k + 1) * C],
                    start=True,
                    stop=True,
                )

        gated = [held.tile([P, E * C], F32, name=f"gated{i}") for i in range(TILES - 1)]
        last = {}

        def weigh(g, i, tag=None):
            e0, count = GROUPS[g]
            if i == TILES - 1:
                last[g] = held.tile([P, count * C], F32, name=f"last{g}", tag=tag or f"last{g}", align_bytes=64)
                target = last[g][:]
            else:
                target = gated[i][:, e0 * C : (e0 + count) * C]
            nc.vector.tensor_tensor(target, sums[g, i][:, 0 : count * C], gates[g][:], MULT)

        def scatter_scalar(i, s0, s1):
            nc.scalar.activation(windows[i][:].indirect(listed(s0, s1 - s0)), gated[i][:, s0:s1], COPY)

        def scatter_vector(i, s0, s1):
            nc.vector.tensor_copy(windows[i][:].indirect(listed(s0, s1 - s0)), gated[i][:, s0:s1])

        quantise(0)
        woven[1] = held.tile([P, 3 * C, PACK], BF16, name="woven1", tag="woven", align_bytes=64)
        by_slot = flat[1][:].rearrange("p j s -> p s j")
        nc.vector.tensor_copy(woven[1][:, 0:WOVEN, :], by_slot[:, 0:WOVEN, :])
        nc.scalar.copy(woven[1][:, WOVEN:, :], by_slot[:, WOVEN:, :])
        for i in (0, 1, 3, 2):
            multiply(0, i, i)
        weigh(0, 0)
        scatter_scalar(0, 0, 2 * C)
        weigh(0, 1)
        scatter_scalar(1, 0, 2 * C)
        weigh(0, 3)
        quantise(1)
        woven[2] = held.tile([P, 3 * C, PACK], BF16, name="woven2", tag="woven", align_bytes=64)
        nc.gpsimd.tensor_scalar(woven[2][:], flat[2][:].rearrange("p j s -> p s j"), 1.0, 0.0, MULT, ADD)
        weigh(0, 2)
        scatter_vector(2, 0, FILL)
        for i in (1, 0, 3, 2):
            multiply(1, i, TILES + i)
        weigh(1, 1)
        scatter_scalar(1, 2 * C, E * C - SHARE)
        weigh(1, 0)
        scatter_scalar(0, 2 * C, 5 * C)
        quantise(2)
        weigh(1, 3, "woven")
        weigh(1, 2)
        for i in range(TILES):
            multiply(2, i, i)
        windows[3] = held.tile([P, T], F32, name="window3", tag="codes", align_bytes=64)
        nc.gpsimd.memset(windows[3][:], 0.0)
        weigh(2, 0)
        scatter_scalar(0, 5 * C, E * C)
        weigh(2, 1)
        scatter_vector(1, E * C - SHARE, E * C)
        weigh(2, 2)
        weigh(2, 3)
        for g, (e0, count) in enumerate(GROUPS):
            nc.scalar.activation(windows[3][:].indirect(listed(e0 * C, count * C)), last[g][:], COPY)
        scatter_vector(2, FILL, E * C)

        for i in (1, 0):
            total = held.tile([P, T], F32, name=f"total{i}")
            for h in range(2):
                cols = slice(h * HALF, (h + 1) * HALF)
                nc.gpsimd.tensor_tensor(total[:, cols], windows[i][:, cols], residual[i, h][:], ADD)
                nc.sync.dma_start(out[i * P : (i + 1) * P, cols], total[:, cols])
        for i, tag in ((2, "xr0_1"), (3, "xr2_0")):
            total = held.tile([P, T], F32, name=f"total{i}", tag=tag)
            for t0 in range(0, T, PIECE):
                cols = slice(t0, t0 + PIECE)
                h = t0 // HALF
                part = residual[i, h][:, t0 - h * HALF : t0 - h * HALF + PIECE]
                nc.vector.tensor_tensor(total[:, cols], windows[i][:, cols], part, ADD)
                nc.sync.dma_start(out[i * P : (i + 1) * P, cols], total[:, cols])
